import numpy as np
import ml_dtypes


def mxq(x, axis, fmt="e4m3"):
    dtype, down = {"e4m3": (ml_dtypes.float8_e4m3fn, 7), "e5m2": (ml_dtypes.float8_e5m2, 14)}[fmt]
    v = np.moveaxis(np.asarray(x, np.float32).astype(ml_dtypes.bfloat16).astype(np.float64), axis, -1)
    blocks = v.reshape(v.shape[:-1] + (-1, 32))
    amax = np.abs(blocks).max(-1, keepdims=True)
    byte = np.maximum(np.where(amax > 0, np.frexp(amax)[1] - 1 + 127, 0) - down, 1)
    scale = np.exp2(byte - 127.0)
    codes = (blocks / scale).astype(np.float32).astype(dtype).astype(np.float64)
    return np.moveaxis((codes * scale).reshape(v.shape), -1, axis)


WIDE = False


def mx_kscale(k):
    if not WIDE:
        return np.ones(k)
    levels = np.array([10, -10, 5, -5, 0])
    if k % 512:
        return np.exp2(np.random.permutation(np.resize(levels, k // 32))).repeat(32)
    a = np.empty((k // 512, 16))
    for p in range(k // 512):
        a[p, :8] = np.random.permutation(np.resize(levels, 8))
        for g in range(8):
            far = levels[np.abs(levels - a[p, g]) >= 10]
            a[p, g + 8] = far[np.random.randint(len(far))]
    return np.exp2(a.ravel()).repeat(32)


def f64(x):
    return np.asarray(x).astype(np.float64)


def striped(idx):
    return np.tile(idx.reshape(-1, 16).T, (8, 1)).astype(np.uint16)


def unstriped(offs):
    return offs[:16].T.reshape(-1).astype(np.int64)


E2M1 = np.array([0.0, 0.5, 1.0, 1.5, 2.0, 3.0, 4.0, 6.0, -0.0, -0.5, -1.0, -1.5, -2.0, -3.0, -4.0, -6.0])


def pack_fp4(w):
    k, n = w.shape
    w = f64(np.asarray(w, np.float32).astype(ml_dtypes.bfloat16)).reshape(k // 32, 32, n)
    amax = np.abs(w).max(1)
    mant, ex = np.frexp(amax / 6.0)
    byte = np.clip(np.where(amax > 0, np.where(mant > 0.5, ex, ex - 1) + 127, 1), 1, 254)
    scaled = (w * np.exp2(127.0 - byte)[:, None, :]).reshape(k, n).astype(np.float32)
    c = np.ascontiguousarray(scaled.reshape(k // 512, 128, 4, n).transpose(0, 1, 3, 2)).astype(ml_dtypes.float4_e2m1fn).view(np.uint8) & 0xF
    words = (c[..., 0::2] | (c[..., 1::2] << 4)).reshape(k // 512, 128, 2 * n)
    return np.ascontiguousarray(words), np.ascontiguousarray(byte.astype(np.uint8).reshape(k // 512, 16, n))


def unpack_fp4(words, scales):
    g, _, n = scales.shape
    words = np.ascontiguousarray(words).reshape(g, 128, n, 2)
    nib = np.empty((g, 128, n, 4), np.uint8)
    nib[..., 0::2] = words & 0xF
    nib[..., 1::2] = words >> 4
    vals = E2M1[nib] * np.repeat(np.exp2(scales.astype(np.float64) - 127.0), 8, axis=1)[..., None]
    return vals.transpose(0, 1, 3, 2).reshape(g * 512, n)


def relu(v):
    return np.maximum(v, 0.0)


K, T, S, V, N = 512, 4096, 1536, 384, 256


def setup_inputs():
    n = np.random.standard_normal
    s = mx_kscale(K)[:, None]
    packed_w1 = pack_fp4(n((K, N)) / np.sqrt(K) / s)
    packed_w2 = pack_fp4(n((K, N)) / np.sqrt(K) / s)
    return {
        "xT": (n((K, T)) * s).astype(np.float32),
        "w1_words": packed_w1[0],
        "w1_scales": packed_w1[1],
        "w2_words": packed_w2[0],
        "w2_scales": packed_w2[1],
        "offs": striped(np.random.permutation(T)[:S]),
    }


def reference(xT, w1_words, w1_scales, w2_words, w2_scales, offs):
    xq = mxq(f64(xT)[:, unstriped(offs)], 0, "e4m3")
    e = np.exp(unpack_fp4(w1_words, w1_scales).T @ xq)
    h = unpack_fp4(w2_words, w2_scales).T @ xq
    num = e[:, :V] * h[:, :V] + e[:, V:2 * V] * h[:, V:2 * V] + e[:, 2 * V:3 * V] * h[:, 2 * V:3 * V] + e[:, 3 * V:4 * V] * h[:, 3 * V:4 * V]
    den = e[:, :V] + e[:, V:2 * V] + e[:, 2 * V:3 * V] + e[:, 3 * V:4 * V]
    return relu(num / den)

@@ -1,0 +1,155 @@
+from contextlib import ExitStack
+
+import concourse.mybir as mybir
+from concourse.masks import make_identity
+
+K, T, S, V, N = 512, 4096, 1536, 384, 256
+D = S // V
+FLOPS = 2 * 2 * K * N * S
+
+F32 = mybir.dt.float32
+BF16 = mybir.dt.bfloat16
+I32 = mybir.dt.int32
+U32 = mybir.dt.uint32
+U16 = mybir.dt.uint16
+U8 = mybir.dt.uint8
+FP8X4 = mybir.dt.float8_e4m3fn_x4
+FP4X4 = mybir.dt.float4_e2m1fn_x4
+ALU = mybir.AluOpType
+ACT = mybir.ActivationFunctionType
+
+P = 128
+PACK = 4
+HALF = S // 2
+V_TILES = V // P
+M_TILES = N // P
+
+LOAD_ORDER = (0, 2, 1, 3)
+LOAD_WIDTHS = {
+    0: (2048, 2048),
+    2: (1024, 1024, 1024, 1024),
+    1: (2048, 2048),
+    3: (1024, 1024, 512, 512, 512, 512),
+}
+SHARED_ROWS = (2, 3)
+
+
+def tile_picked_apool_relu_e_kernel(
+    tc, xT, w1_words, w1_scales, w2_words, w2_scales, offs, out
+):
+    nc = tc.nc
+    with ExitStack() as ctx:
+        keep = ctx.enter_context(tc.tile_pool(name="keep", bufs=1))
+        work = ctx.enter_context(tc.tile_pool(name="work", bufs=2))
+        products = ctx.enter_context(tc.psum_pool(name="products", bufs=4))
+        sums = ctx.enter_context(tc.psum_pool(name="sums", bufs=4))
+
+        offsets = keep.tile([P, S // 16], U16, name="offsets")
+        nc.sync.dma_start(offsets[:], offs)
+
+        w_words = keep.tile([P, 2, 2 * N], U8, name="w_words", align_bytes=64)
+        w_scales = keep.tile([P, 2 * N], U8, name="w_scales", align_bytes=64)
+        nc.gpsimd.memset(w_scales[:].bitcast(I32), 0)
+        for w, (words, scales) in enumerate(((w1_words, w1_scales), (w2_words, w2_scales))):
+            nc.gpsimd.dma_start(w_words[:, w, :].bitcast(I32), words[0].bitcast(I32))
+            for q in range(4):
+                nc.gpsimd.dma_start(
+                    w_scales[32 * q : 32 * q + 4, w * N : (w + 1) * N].bitcast(I32),
+                    scales[0, 4 * q : 4 * q + 4, :].bitcast(I32),
+                )
+        identity = keep.tile([P, P], F32, name="identity")
+        make_identity(nc, identity[:])
+
+        x_rows = xT.rearrange("(p j) t -> j p t", j=PACK)
+        picked = [
+            keep.tile([P, HALF, PACK], BF16, name="picked%d" % half, align_bytes=64)
+            for half in range(2)
+        ]
+        half_offsets = [offsets[:, half * HALF // 16 : (half + 1) * HALF // 16] for half in range(2)]
+        for j in LOAD_ORDER:
+            row = keep.tile([P, T], F32, name="row%d" % j)
+            if j in SHARED_ROWS:
+                row_bf16 = keep.tile([P, T], BF16, name="row_bf16_%d" % j)
+            first = 0
+            for width in LOAD_WIDTHS[j]:
+                cols = slice(first, first + width)
+                nc.sync.dma_start(row[:, cols], x_rows[j][:, cols])
+                if j in SHARED_ROWS:
+                    nc.scalar.activation(row_bf16[:, cols], row[:, cols], ACT.Copy)
+                first = first + width
+            nc.vector.tensor_copy(picked[0][:, :, j], row[:].indirect(half_offsets[0]))
+            if j in SHARED_ROWS:
+                nc.scalar.activation(picked[1][:, :, j], row_bf16[:].indirect(half_offsets[1]), ACT.Copy)
+            else:
+                nc.vector.tensor_copy(picked[1][:, :, j], row[:].indirect(half_offsets[1]))
+
+        codes = {}
+        code_scales = {}
+        for vt in range(V_TILES):
+            for d in range(D):
+                half, first = divmod(d * V + vt * P, HALF)
+                codes[vt, d] = keep.tile([P, P], U32, name="codes%d_%d" % (vt, d), align_bytes=64)
+                code_scales[vt, d] = keep.tile([P, P], U8, name="code_scales%d_%d" % (vt, d), align_bytes=64)
+                nc.vector.quantize_mx(
+                    out=codes[vt, d][:].bitcast(FP8X4),
+                    scales=code_scales[vt, d][:],
+                    in_=picked[half][:, first : first + P, :].rearrange("p n j -> p (n j)"),
+                )
+
+        def product(w, vt, mt):
+            bank = products.tile([P, D, P], F32, name="product")
+            for d in range(D):
+                nc.tensor.matmul_mx(
+                    out=bank[:, d, :],
+                    lhsT=codes[vt, d][:].bitcast(FP8X4),
+                    lhsT_scale=code_scales[vt, d][:],
+                    rhs=w_words[:, w, 2 * P * mt : 2 * P * (mt + 1)].bitcast(FP4X4),
+                    rhs_scale=w_scales[:, w * N + P * mt : w * N + P * (mt + 1)],
+                    start=True,
+                    stop=True,
+                )
+            return bank
+
+        def sum_transposed(total, terms):
+            for d in range(D):
+                nc.tensor.matmul(
+                    total, lhsT=terms[:, d, :], rhs=identity[:], is_transpose=True,
+                    start=(d == 0), stop=(d == D - 1),
+                )
+
+        weights = {}
+        den_squared = keep.tile([P, V_TILES, M_TILES * P], F32, name="den_squared")
+        for vt in range(V_TILES):
+            den = sums.tile([P, M_TILES, P], F32, name="total")
+            for mt in range(M_TILES):
+                scores = product(0, vt, mt)
+                largest = work.tile([P, P], F32, name="largest")
+                nc.vector.tensor_reduce(
+                    largest[:], scores[:].rearrange("p d m -> p m d"), mybir.AxisListType.X, ALU.max
+                )
+                shifted = work.tile([P, D, P], F32, name="shifted")
+                nc.vector.tensor_tensor(
+                    shifted[:], scores[:], largest[:].unsqueeze(1).broadcast_to([P, D, P]), ALU.subtract
+                )
+                weights[vt, mt] = keep.tile([P, D, P], F32, name="weights%d_%d" % (vt, mt))
+                nc.scalar.activation(weights[vt, mt][:], shifted[:], ACT.Exp)
+                sum_transposed(den[:, mt, :], weights[vt, mt])
+            nc.scalar.activation(den_squared[:, vt, :], den[:].rearrange("p a b -> p (a b)"), ACT.Square)
+
+        inverse = keep.tile([P, V_TILES, M_TILES * P], F32, name="inverse")
+        nc.scalar.activation(inverse[:], den_squared[:], ACT.Abs_reciprocal_sqrt)
+
+        out_tiles = out.rearrange("(mt p) v -> p mt v", p=P)
+        for vt in range(V_TILES):
+            num = sums.tile([P, M_TILES, P], F32, name="total")
+            for mt in range(M_TILES):
+                values = product(1, vt, mt)
+                weighted = work.tile([P, D, P], F32, name="weighted")
+                nc.vector.tensor_tensor(weighted[:], values[:], weights[vt, mt][:], ALU.mult)
+                sum_transposed(num[:, mt, :], weighted)
+            result = keep.tile([P, M_TILES, P], F32, name="result%d" % vt)
+            nc.vector.scalar_tensor_tensor(
+                result[:].rearrange("p a b -> p (a b)"), num[:].rearrange("p a b -> p (a b)"), 0.0,
+                inverse[:, vt, :], ALU.max, ALU.mult,
+            )
+            nc.sync.dma_start(out_tiles[:, :, vt * P : (vt + 1) * P], result[:])

@@ -20,18 +20,17 @@ ACT = mybir.ActivationFunctionType
 
 P = 128
 PACK = 4
-HALF = S // 2
 V_TILES = V // P
 M_TILES = N // P
 
-LOAD_ORDER = (0, 2, 1, 3)
-LOAD_WIDTHS = {
-    0: (2048, 2048),
-    2: (1024, 1024, 1024, 1024),
-    1: (2048, 2048),
-    3: (1024, 1024, 512, 512, 512, 512),
-}
-SHARED_ROWS = (2, 3)
+LOAD_WIDTHS = (
+    (1024, 1024, 1024, 1024),
+    (1024, 1024, 1024, 1024),
+    (1024, 1024, 1024, 1024),
+    (1024, 1024, 1024, 512, 512),
+)
+VECTOR_SHARE = 704
+EARLY_VALUES = 2
 
 
 def tile_picked_apool_relu_e_kernel(
@@ -40,60 +39,58 @@ def tile_picked_apool_relu_e_kernel(
     nc = tc.nc
     with ExitStack() as ctx:
         keep = ctx.enter_context(tc.tile_pool(name="keep", bufs=1))
-        work = ctx.enter_context(tc.tile_pool(name="work", bufs=2))
-        products = ctx.enter_context(tc.psum_pool(name="products", bufs=4))
-        sums = ctx.enter_context(tc.psum_pool(name="sums", bufs=4))
+        work = ctx.enter_context(tc.tile_pool(name="work", bufs=3))
+        products = ctx.enter_context(tc.psum_pool(name="products", bufs=5))
+        sums = ctx.enter_context(tc.psum_pool(name="sums", bufs=1))
 
         offsets = keep.tile([P, S // 16], U16, name="offsets")
         nc.sync.dma_start(offsets[:], offs)
+
+        identity = keep.tile([P, P], F32, name="identity")
+        make_identity(nc, identity[:])
 
         w_words = keep.tile([P, 2, 2 * N], U8, name="w_words", align_bytes=64)
         w_scales = keep.tile([P, 2 * N], U8, name="w_scales", align_bytes=64)
         nc.gpsimd.memset(w_scales[:].bitcast(I32), 0)
         for w, (words, scales) in enumerate(((w1_words, w1_scales), (w2_words, w2_scales))):
-            nc.gpsimd.dma_start(w_words[:, w, :].bitcast(I32), words[0].bitcast(I32))
+            nc.scalar.dma_start(w_words[:, w, :].bitcast(I32), words[0].bitcast(I32))
             for q in range(4):
                 nc.gpsimd.dma_start(
                     w_scales[32 * q : 32 * q + 4, w * N : (w + 1) * N].bitcast(I32),
                     scales[0, 4 * q : 4 * q + 4, :].bitcast(I32),
                 )
-        identity = keep.tile([P, P], F32, name="identity")
-        make_identity(nc, identity[:])
 
         x_rows = xT.rearrange("(p j) t -> j p t", j=PACK)
-        picked = [
-            keep.tile([P, HALF, PACK], BF16, name="picked%d" % half, align_bytes=64)
-            for half in range(2)
-        ]
-        half_offsets = [offsets[:, half * HALF // 16 : (half + 1) * HALF // 16] for half in range(2)]
-        for j in LOAD_ORDER:
+        picked = keep.tile([P, S, PACK], BF16, name="picked", align_bytes=64)
+        for j in range(PACK):
             row = keep.tile([P, T], F32, name="row%d" % j)
-            if j in SHARED_ROWS:
-                row_bf16 = keep.tile([P, T], BF16, name="row_bf16_%d" % j)
+            row_bf16 = keep.tile([P, T], BF16, name="row_bf16_%d" % j)
             first = 0
             for width in LOAD_WIDTHS[j]:
                 cols = slice(first, first + width)
                 nc.sync.dma_start(row[:, cols], x_rows[j][:, cols])
-                if j in SHARED_ROWS:
-                    nc.scalar.activation(row_bf16[:, cols], row[:, cols], ACT.Copy)
+                nc.vector.tensor_copy(row_bf16[:, cols], row[:, cols])
                 first = first + width
-            nc.vector.tensor_copy(picked[0][:, :, j], row[:].indirect(half_offsets[0]))
-            if j in SHARED_ROWS:
-                nc.scalar.activation(picked[1][:, :, j], row_bf16[:].indirect(half_offsets[1]), ACT.Copy)
-            else:
-                nc.vector.tensor_copy(picked[1][:, :, j], row[:].indirect(half_offsets[1]))
+            nc.vector.tensor_copy(
+                picked[:, 0:VECTOR_SHARE, j], row[:].indirect(offsets[:, 0 : VECTOR_SHARE // 16])
+            )
+            nc.scalar.activation(
+                picked[:, VECTOR_SHARE:S, j],
+                row_bf16[:].indirect(offsets[:, VECTOR_SHARE // 16 : S // 16]),
+                ACT.Copy,
+            )
 
         codes = {}
         code_scales = {}
         for vt in range(V_TILES):
             for d in range(D):
-                half, first = divmod(d * V + vt * P, HALF)
+                first = d * V + vt * P
                 codes[vt, d] = keep.tile([P, P], U32, name="codes%d_%d" % (vt, d), align_bytes=64)
                 code_scales[vt, d] = keep.tile([P, P], U8, name="code_scales%d_%d" % (vt, d), align_bytes=64)
                 nc.vector.quantize_mx(
                     out=codes[vt, d][:].bitcast(FP8X4),
                     scales=code_scales[vt, d][:],
-                    in_=picked[half][:, first : first + P, :].rearrange("p n j -> p (n j)"),
+                    in_=picked[:, first : first + P, :].rearrange("p n j -> p (n j)"),
                 )
 
         def product(w, vt, mt):
@@ -110,46 +107,72 @@ def tile_picked_apool_relu_e_kernel(
                 )
             return bank
 
-        def sum_transposed(total, terms):
-            for d in range(D):
+        def sum_transposed(total, terms, count):
+            for d in range(count):
                 nc.tensor.matmul(
                     total, lhsT=terms[:, d, :], rhs=identity[:], is_transpose=True,
-                    start=(d == 0), stop=(d == D - 1),
+                    start=(d == 0), stop=(d == count - 1),
                 )
 
+        def sum_pairs_first(total, terms):
+            pairs = work.tile([P, D // 2, P], F32, name="pairs")
+            nc.gpsimd.tensor_tensor(pairs[:], terms[:, 0 : D // 2, :], terms[:, D // 2 : D, :], ALU.add)
+            sum_transposed(total, pairs, D // 2)
+
+        units = [(vt, mt) for vt in range(V_TILES) for mt in range(M_TILES)]
         weights = {}
-        den_squared = keep.tile([P, V_TILES, M_TILES * P], F32, name="den_squared")
-        for vt in range(V_TILES):
-            den = sums.tile([P, M_TILES, P], F32, name="total")
-            for mt in range(M_TILES):
-                scores = product(0, vt, mt)
-                largest = work.tile([P, P], F32, name="largest")
-                nc.vector.tensor_reduce(
-                    largest[:], scores[:].rearrange("p d m -> p m d"), mybir.AxisListType.X, ALU.max
-                )
-                shifted = work.tile([P, D, P], F32, name="shifted")
-                nc.vector.tensor_tensor(
-                    shifted[:], scores[:], largest[:].unsqueeze(1).broadcast_to([P, D, P]), ALU.subtract
-                )
-                weights[vt, mt] = keep.tile([P, D, P], F32, name="weights%d_%d" % (vt, mt))
-                nc.scalar.activation(weights[vt, mt][:], shifted[:], ACT.Exp)
-                sum_transposed(den[:, mt, :], weights[vt, mt])
-            nc.scalar.activation(den_squared[:, vt, :], den[:].rearrange("p a b -> p (a b)"), ACT.Square)
+        values = {}
+        dens = {}
+        den_squared = keep.tile([P, M_TILES, V_TILES, P], F32, name="den_squared")
+        last = V_TILES - 1
+        for u, (vt, mt) in enumerate(units):
+            if mt == 0:
+                dens[vt] = sums.tile([P, M_TILES, P], F32, name="den%d" % vt, tag="sums%d" % vt)
+            scores = product(0, vt, mt)
+            if 1 <= u <= EARLY_VALUES:
+                values[units[u - 1]] = product(1, *units[u - 1])
+            largest = work.tile([P, P], F32, name="largest")
+            nc.vector.tensor_reduce(
+                largest[:], scores[:].rearrange("p d m -> p m d"), mybir.AxisListType.X, ALU.max
+            )
+            shifted = work.tile([P, D, P], F32, name="shifted")
+            nc.vector.tensor_tensor(
+                shifted[:], scores[:], largest[:].unsqueeze(1).broadcast_to([P, D, P]), ALU.subtract
+            )
+            weights[vt, mt] = keep.tile([P, D, P], F32, name="weights%d_%d" % (vt, mt))
+            nc.scalar.activation(weights[vt, mt][:], shifted[:], ACT.Exp)
+            sum_transposed(dens[vt][:, mt, :], weights[vt, mt], D)
+            if mt == M_TILES - 1 and vt < last:
+                nc.scalar.activation(den_squared[:, :, vt, :], dens[vt][:], ACT.Square)
 
-        inverse = keep.tile([P, V_TILES, M_TILES * P], F32, name="inverse")
-        nc.scalar.activation(inverse[:], den_squared[:], ACT.Abs_reciprocal_sqrt)
+        inverse_early = shifted[:].rearrange("p (mt vt) v -> p mt vt v", mt=M_TILES)
+        nc.scalar.activation(inverse_early, den_squared[:, :, 0:last, :], ACT.Abs_reciprocal_sqrt)
+        nc.scalar.activation(den_squared[:, :, last, :], dens[last][:], ACT.Square)
+        inverse_last = keep.tile([P, M_TILES, P], F32, name="inverse_last")
+        nc.scalar.activation(inverse_last[:], den_squared[:, :, last, :], ACT.Abs_reciprocal_sqrt)
+
+        num_early = sums.tile([P, M_TILES, last, P], F32, name="num_early", tag="sums0")
+        num_last = sums.tile([P, M_TILES, P], F32, name="num_last", tag="sums1")
+        for unit in units[EARLY_VALUES:]:
+            values[unit] = product(1, *unit)
+        for vt, mt in units:
+            weighted = work.tile([P, D, P], F32, name="weighted")
+            nc.vector.tensor_tensor(weighted[:], values[vt, mt][:], weights[vt, mt][:], ALU.mult)
+            if vt < last:
+                sum_transposed(num_early[:, mt, vt, :], weighted, D)
+            else:
+                sum_transposed(num_last[:, mt, :], weighted, D)
 
         out_tiles = out.rearrange("(mt p) v -> p mt v", p=P)
-        for vt in range(V_TILES):
-            num = sums.tile([P, M_TILES, P], F32, name="total")
-            for mt in range(M_TILES):
-                values = product(1, vt, mt)
-                weighted = work.tile([P, D, P], F32, name="weighted")
-                nc.vector.tensor_tensor(weighted[:], values[:], weights[vt, mt][:], ALU.mult)
-                sum_transposed(num[:, mt, :], weighted)
-            result = keep.tile([P, M_TILES, P], F32, name="result%d" % vt)
-            nc.vector.scalar_tensor_tensor(
-                result[:].rearrange("p a b -> p (a b)"), num[:].rearrange("p a b -> p (a b)"), 0.0,
-                inverse[:, vt, :], ALU.max, ALU.mult,
-            )
-            nc.sync.dma_start(out_tiles[:, :, vt * P : (vt + 1) * P], result[:])
+        result_early = keep.tile([P, M_TILES, last * P], F32, name="result_early")
+        nc.vector.scalar_tensor_tensor(
+            result_early[:].rearrange("p a b -> p (a b)"), num_early[:].rearrange("p a b c -> p (a b c)"), 0.0,
+            inverse_early.rearrange("p a b c -> p (a b c)"), ALU.max, ALU.mult,
+        )
+        nc.sync.dma_start(out_tiles[:, :, 0 : last * P], result_early[:])
+        result_last = keep.tile([P, M_TILES, P], F32, name="result_last")
+        nc.vector.scalar_tensor_tensor(
+            result_last[:].rearrange("p a b -> p (a b)"), num_last[:].rearrange("p a b -> p (a b)"), 0.0,
+            inverse_last[:].rearrange("p a b -> p (a b)"), ALU.max, ALU.mult,
+        )
+        nc.sync.dma_start(out_tiles[:, :, last * P : V], result_last[:])

@@ -24,12 +24,13 @@ V_TILES = V // P
 M_TILES = N // P
 
 LOAD_WIDTHS = (
-    (1024, 1024, 1024, 1024),
-    (1024, 1024, 1024, 1024),
-    (1024, 1024, 1024, 1024),
-    (1024, 1024, 1024, 512, 512),
+    (2048, 2048),
+    (2048, 2048),
+    (2048, 1024, 1024),
+    (2048, 1024, 512, 256, 256),
 )
-VECTOR_SHARE = 704
+LOAD_ORDER = (2, 0, 1, 3)
+VECTOR_SHARES = (512, 512, 768, 768)
 EARLY_VALUES = 2
 
 
@@ -62,28 +63,28 @@ def tile_picked_apool_relu_e_kernel(
 
         x_rows = xT.rearrange("(p j) t -> j p t", j=PACK)
         picked = keep.tile([P, S, PACK], BF16, name="picked", align_bytes=64)
-        for j in range(PACK):
+        for j, widths in zip(LOAD_ORDER, LOAD_WIDTHS):
             row = keep.tile([P, T], F32, name="row%d" % j)
             row_bf16 = keep.tile([P, T], BF16, name="row_bf16_%d" % j)
             first = 0
-            for width in LOAD_WIDTHS[j]:
+            for width in widths:
                 cols = slice(first, first + width)
                 nc.sync.dma_start(row[:, cols], x_rows[j][:, cols])
-                nc.vector.tensor_copy(row_bf16[:, cols], row[:, cols])
                 first = first + width
-            nc.vector.tensor_copy(
-                picked[:, 0:VECTOR_SHARE, j], row[:].indirect(offsets[:, 0 : VECTOR_SHARE // 16])
-            )
+                if j == PACK - 1 and first == T:
+                    nc.scalar.copy(row_bf16[:, cols], row[:, cols])
+                else:
+                    nc.vector.tensor_copy(row_bf16[:, cols], row[:, cols])
+            share = VECTOR_SHARES[j]
+            nc.vector.tensor_copy(picked[:, 0:share, j], row[:].indirect(offsets[:, 0 : share // 16]))
             nc.scalar.activation(
-                picked[:, VECTOR_SHARE:S, j],
-                row_bf16[:].indirect(offsets[:, VECTOR_SHARE // 16 : S // 16]),
-                ACT.Copy,
+                picked[:, share:S, j], row_bf16[:].indirect(offsets[:, share // 16 : S // 16]), ACT.Copy
             )
 
         codes = {}
         code_scales = {}
-        for vt in range(V_TILES):
-            for d in range(D):
+        for half in range(2):
+            for vt, d in [(vt, d) for vt in range(V_TILES) for d in (2 * half, 2 * half + 1)]:
                 first = d * V + vt * P
                 codes[vt, d] = keep.tile([P, P], U32, name="codes%d_%d" % (vt, d), align_bytes=64)
                 code_scales[vt, d] = keep.tile([P, P], U8, name="code_scales%d_%d" % (vt, d), align_bytes=64)

@@ -30,8 +30,9 @@ LOAD_WIDTHS = (
     (2048, 1024, 512, 256, 256),
 )
 LOAD_ORDER = (2, 0, 1, 3)
+GPSIMD_PRODUCTS = ((0, 0),)
+QUANTISE_RUNS = ((0, 256), (256, 512), (768, 128), (1152, 128), (896, 256), (1280, 256))
 VECTOR_SHARES = (512, 512, 768, 768)
-EARLY_VALUES = 2
 
 
 def tile_picked_apool_relu_e_kernel(
@@ -40,12 +41,9 @@ def tile_picked_apool_relu_e_kernel(
     nc = tc.nc
     with ExitStack() as ctx:
         keep = ctx.enter_context(tc.tile_pool(name="keep", bufs=1))
-        work = ctx.enter_context(tc.tile_pool(name="work", bufs=3))
-        products = ctx.enter_context(tc.psum_pool(name="products", bufs=5))
-        sums = ctx.enter_context(tc.psum_pool(name="sums", bufs=1))
+        banks = ctx.enter_context(tc.psum_pool(name="banks", bufs=1))
 
         offsets = keep.tile([P, S // 16], U16, name="offsets")
-        nc.sync.dma_start(offsets[:], offs)
 
         identity = keep.tile([P, P], F32, name="identity")
         make_identity(nc, identity[:])
@@ -53,8 +51,7 @@ def tile_picked_apool_relu_e_kernel(
         w_words = keep.tile([P, 2, 2 * N], U8, name="w_words", align_bytes=64)
         w_scales = keep.tile([P, 2 * N], U8, name="w_scales", align_bytes=64)
         nc.gpsimd.memset(w_scales[:].bitcast(I32), 0)
-        for w, (words, scales) in enumerate(((w1_words, w1_scales), (w2_words, w2_scales))):
-            nc.scalar.dma_start(w_words[:, w, :].bitcast(I32), words[0].bitcast(I32))
+        for w, scales in enumerate((w1_scales, w2_scales)):
             for q in range(4):
                 nc.gpsimd.dma_start(
                     w_scales[32 * q : 32 * q + 4, w * N : (w + 1) * N].bitcast(I32),
@@ -70,6 +67,8 @@ def tile_picked_apool_relu_e_kernel(
             for width in widths:
                 cols = slice(first, first + width)
                 nc.sync.dma_start(row[:, cols], x_rows[j][:, cols])
+                if j == LOAD_ORDER[0] and first == 0:
+                    nc.sync.dma_start(offsets[:], offs)
                 first = first + width
                 if j == PACK - 1 and first == T:
                     nc.scalar.copy(row_bf16[:, cols], row[:, cols])
@@ -81,94 +80,135 @@ def tile_picked_apool_relu_e_kernel(
                 picked[:, share:S, j], row_bf16[:].indirect(offsets[:, share // 16 : S // 16]), ACT.Copy
             )
 
+        for w, words in enumerate((w1_words, w2_words)):
+            nc.sync.dma_start(w_words[:, w, :].bitcast(I32), words[0].bitcast(I32))
+
         codes = {}
         code_scales = {}
-        for half in range(2):
-            for vt, d in [(vt, d) for vt in range(V_TILES) for d in (2 * half, 2 * half + 1)]:
-                first = d * V + vt * P
-                codes[vt, d] = keep.tile([P, P], U32, name="codes%d_%d" % (vt, d), align_bytes=64)
-                code_scales[vt, d] = keep.tile([P, P], U8, name="code_scales%d_%d" % (vt, d), align_bytes=64)
-                nc.vector.quantize_mx(
-                    out=codes[vt, d][:].bitcast(FP8X4),
-                    scales=code_scales[vt, d][:],
-                    in_=picked[:, first : first + P, :].rearrange("p n j -> p (n j)"),
-                )
+        for first, count in QUANTISE_RUNS:
+            run_codes = keep.tile([P, count], U32, name="codes%d" % first, align_bytes=64)
+            run_scales = keep.tile([P, count], U8, name="code_scales%d" % first, align_bytes=64)
+            nc.vector.quantize_mx(
+                out=run_codes[:].bitcast(FP8X4),
+                scales=run_scales[:],
+                in_=picked[:, first : first + count, :].rearrange("p n j -> p (n j)"),
+            )
+            for entry in range(first, first + count, P):
+                cols = slice(entry - first, entry - first + P)
+                codes[entry % V // P, entry // V] = run_codes[:, cols]
+                code_scales[entry % V // P, entry // V] = run_scales[:, cols]
 
-        def product(w, vt, mt):
-            bank = products.tile([P, D, P], F32, name="product")
-            for d in range(D):
+        def product(bank, w, vt, mt, pieces):
+            for d in pieces:
                 nc.tensor.matmul_mx(
                     out=bank[:, d, :],
-                    lhsT=codes[vt, d][:].bitcast(FP8X4),
-                    lhsT_scale=code_scales[vt, d][:],
+                    lhsT=codes[vt, d].bitcast(FP8X4),
+                    lhsT_scale=code_scales[vt, d],
                     rhs=w_words[:, w, 2 * P * mt : 2 * P * (mt + 1)].bitcast(FP4X4),
                     rhs_scale=w_scales[:, w * N + P * mt : w * N + P * (mt + 1)],
                     start=True,
                     stop=True,
                 )
-            return bank
 
-        def sum_transposed(total, terms, count):
-            for d in range(count):
+        def sum_transposed(total, terms):
+            for d in range(D):
                 nc.tensor.matmul(
                     total, lhsT=terms[:, d, :], rhs=identity[:], is_transpose=True,
-                    start=(d == 0), stop=(d == count - 1),
+                    start=(d == 0), stop=(d == D - 1),
                 )
 
-        def sum_pairs_first(total, terms):
-            pairs = work.tile([P, D // 2, P], F32, name="pairs")
-            nc.gpsimd.tensor_tensor(pairs[:], terms[:, 0 : D // 2, :], terms[:, D // 2 : D, :], ALU.add)
-            sum_transposed(total, pairs, D // 2)
+        def unit_bank(name, vt, mt):
+            return banks.tile([P, D, P], F32, name="%s%d_%d" % (name, vt, mt), tag="bank%d_%d" % (vt, mt))
 
         units = [(vt, mt) for vt in range(V_TILES) for mt in range(M_TILES)]
-        weights = {}
-        values = {}
+        last = V_TILES - 1
+        scores = {unit: unit_bank("scores", *unit) for unit in units}
+        for pieces in ((0, 1), (2, 3)):
+            for vt, mt in units:
+                product(scores[vt, mt], 0, vt, mt, pieces)
+
         dens = {}
         den_squared = keep.tile([P, M_TILES, V_TILES, P], F32, name="den_squared")
-        last = V_TILES - 1
-        for u, (vt, mt) in enumerate(units):
-            if mt == 0:
-                dens[vt] = sums.tile([P, M_TILES, P], F32, name="den%d" % vt, tag="sums%d" % vt)
-            scores = product(0, vt, mt)
-            if 1 <= u <= EARLY_VALUES:
-                values[units[u - 1]] = product(1, *units[u - 1])
-            largest = work.tile([P, P], F32, name="largest")
-            nc.vector.tensor_reduce(
-                largest[:], scores[:].rearrange("p d m -> p m d"), mybir.AxisListType.X, ALU.max
-            )
-            shifted = work.tile([P, D, P], F32, name="shifted")
-            nc.vector.tensor_tensor(
-                shifted[:], scores[:], largest[:].unsqueeze(1).broadcast_to([P, D, P]), ALU.subtract
-            )
-            weights[vt, mt] = keep.tile([P, D, P], F32, name="weights%d_%d" % (vt, mt))
-            nc.scalar.activation(weights[vt, mt][:], shifted[:], ACT.Exp)
-            sum_transposed(dens[vt][:, mt, :], weights[vt, mt], D)
-            if mt == M_TILES - 1 and vt < last:
-                nc.scalar.activation(den_squared[:, :, vt, :], dens[vt][:], ACT.Square)
+        shifted_last = keep.tile([P, M_TILES, D, P], F32, name="shifted_last")
+        copied = {}
+        largest = {}
+        weights = {}
+        values = {}
 
-        inverse_early = shifted[:].rearrange("p (mt vt) v -> p mt vt v", mt=M_TILES)
-        nc.scalar.activation(inverse_early, den_squared[:, :, 0:last, :], ACT.Abs_reciprocal_sqrt)
-        nc.scalar.activation(den_squared[:, :, last, :], dens[last][:], ACT.Square)
+        def copy_scores(vt):
+            copied[vt] = keep.tile([P, D, P], F32, name="copied%d" % vt)
+            nc.scalar.copy(copied[vt][:], scores[vt, 0][:])
+
+        def maximum(vt, mt):
+            largest[vt, mt] = keep.tile([P, P], F32, name="largest%d_%d" % (vt, mt))
+            nc.vector.tensor_reduce(
+                largest[vt, mt][:], scores[vt, mt][:].rearrange("p d m -> p m d"), mybir.AxisListType.X, ALU.max
+            )
+
+        def weigh(vt, mt):
+            if vt < last:
+                shifted_tile = keep.tile([P, D, P], F32, name="shifted%d_%d" % (vt, mt))
+                shifted = shifted_tile[:]
+            else:
+                shifted = shifted_last[:, mt, :, :]
+            spread = largest[vt, mt][:].unsqueeze(1).broadcast_to([P, D, P])
+            if mt == 0:
+                nc.gpsimd.tensor_tensor(shifted, copied[vt][:], spread, ALU.subtract)
+            else:
+                nc.vector.tensor_tensor(shifted, scores[vt, mt][:], spread, ALU.subtract)
+            weights[vt, mt] = keep.tile([P, D, P], F32, name="weights%d_%d" % (vt, mt))
+            nc.scalar.activation(weights[vt, mt][:], shifted, ACT.Exp)
+            values[vt, mt] = unit_bank("values", vt, mt)
+            product(values[vt, mt], 1, vt, mt, range(D))
+            if vt not in dens:
+                dens[vt] = banks.tile([P, M_TILES, P], F32, name="den%d" % vt, tag="den%d" % (vt % 2))
+            sum_transposed(dens[vt][:, mt, :], weights[vt, mt])
+
+        for vt in range(V_TILES):
+            copy_scores(vt)
+        def square(vt):
+            nc.scalar.activation(den_squared[:, :, vt, :], dens[vt][:], ACT.Square)
+
+        maximum(0, 1)
+        maximum(0, 0)
+        weigh(0, 1)
+        weigh(0, 0)
+        maximum(1, 0)
+        maximum(1, 1)
+        maximum(2, 0)
+        weigh(1, 0)
+        weigh(1, 1)
+        maximum(2, 1)
+        weigh(2, 0)
+        weigh(2, 1)
+        square(0)
+        square(1)
+        copied_values = {}
+        for unit in GPSIMD_PRODUCTS:
+            copied_values[unit] = keep.tile([P, D, P], F32, name="copied_values%d_%d" % unit)
+            nc.scalar.copy(copied_values[unit][:], values[unit][:])
+
+        held = shifted_last[:].rearrange("p a d m -> p (a d m)")[:, 2 * P : 6 * P]
+        nc.scalar.activation(held.rearrange("p (mt vt v) -> p mt vt v", mt=M_TILES, vt=last), den_squared[:, :, 0:last, :], ACT.Abs_reciprocal_sqrt)
+        square(last)
         inverse_last = keep.tile([P, M_TILES, P], F32, name="inverse_last")
         nc.scalar.activation(inverse_last[:], den_squared[:, :, last, :], ACT.Abs_reciprocal_sqrt)
 
-        num_early = sums.tile([P, M_TILES, last, P], F32, name="num_early", tag="sums0")
-        num_last = sums.tile([P, M_TILES, P], F32, name="num_last", tag="sums1")
-        for unit in units[EARLY_VALUES:]:
-            values[unit] = product(1, *unit)
-        for vt, mt in units:
-            weighted = work.tile([P, D, P], F32, name="weighted")
-            nc.vector.tensor_tensor(weighted[:], values[vt, mt][:], weights[vt, mt][:], ALU.mult)
-            if vt < last:
-                sum_transposed(num_early[:, mt, vt, :], weighted, D)
+        num_early = banks.tile([P, M_TILES, last, P], F32, name="num_early", tag="bank0_0")
+        num_last = banks.tile([P, M_TILES, P], F32, name="num_last", tag="bank0_1")
+        for vt, mt in ((0, 1), (1, 0), (1, 1), (0, 0), (2, 0), (2, 1)):
+            weighted = keep.tile([P, D, P], F32, name="weighted%d_%d" % (vt, mt))
+            if (vt, mt) in copied_values:
+                nc.gpsimd.tensor_tensor(weighted[:], copied_values[vt, mt][:], weights[vt, mt][:], ALU.mult)
             else:
-                sum_transposed(num_last[:, mt, :], weighted, D)
+                nc.vector.tensor_tensor(weighted[:], values[vt, mt][:], weights[vt, mt][:], ALU.mult)
+            sum_transposed(num_early[:, mt, vt, :] if vt < last else num_last[:, mt, :], weighted)
 
         out_tiles = out.rearrange("(mt p) v -> p mt v", p=P)
         result_early = keep.tile([P, M_TILES, last * P], F32, name="result_early")
         nc.vector.scalar_tensor_tensor(
             result_early[:].rearrange("p a b -> p (a b)"), num_early[:].rearrange("p a b c -> p (a b c)"), 0.0,
-            inverse_early.rearrange("p a b c -> p (a b c)"), ALU.max, ALU.mult,
+            held, ALU.max, ALU.mult,
         )
         nc.sync.dma_start(out_tiles[:, :, 0 : last * P], result_early[:])
         result_last = keep.tile([P, M_TILES, P], F32, name="result_last")

@@ -30,7 +30,6 @@ LOAD_WIDTHS = (
     (2048, 1024, 512, 256, 256),
 )
 LOAD_ORDER = (2, 0, 1, 3)
-GPSIMD_PRODUCTS = ((0, 0),)
 QUANTISE_RUNS = ((0, 256), (256, 512), (768, 128), (1152, 128), (896, 256), (1280, 256))
 VECTOR_SHARES = (512, 512, 768, 768)
 
@@ -129,15 +128,10 @@ def tile_picked_apool_relu_e_kernel(
 
         dens = {}
         den_squared = keep.tile([P, M_TILES, V_TILES, P], F32, name="den_squared")
-        shifted_last = keep.tile([P, M_TILES, D, P], F32, name="shifted_last")
-        copied = {}
         largest = {}
+        shifted = {}
         weights = {}
         values = {}
-
-        def copy_scores(vt):
-            copied[vt] = keep.tile([P, D, P], F32, name="copied%d" % vt)
-            nc.scalar.copy(copied[vt][:], scores[vt, 0][:])
 
         def maximum(vt, mt):
             largest[vt, mt] = keep.tile([P, P], F32, name="largest%d_%d" % (vt, mt))
@@ -146,62 +140,42 @@ def tile_picked_apool_relu_e_kernel(
             )
 
         def weigh(vt, mt):
-            if vt < last:
-                shifted_tile = keep.tile([P, D, P], F32, name="shifted%d_%d" % (vt, mt))
-                shifted = shifted_tile[:]
-            else:
-                shifted = shifted_last[:, mt, :, :]
+            shifted[vt, mt] = keep.tile([P, D, P], F32, name="shifted%d_%d" % (vt, mt))
             spread = largest[vt, mt][:].unsqueeze(1).broadcast_to([P, D, P])
-            if mt == 0:
-                nc.gpsimd.tensor_tensor(shifted, copied[vt][:], spread, ALU.subtract)
-            else:
-                nc.vector.tensor_tensor(shifted, scores[vt, mt][:], spread, ALU.subtract)
+            nc.vector.tensor_tensor(shifted[vt, mt][:], scores[vt, mt][:], spread, ALU.subtract)
             weights[vt, mt] = keep.tile([P, D, P], F32, name="weights%d_%d" % (vt, mt))
-            nc.scalar.activation(weights[vt, mt][:], shifted, ACT.Exp)
+            nc.scalar.activation(weights[vt, mt][:], shifted[vt, mt][:], ACT.Exp)
             values[vt, mt] = unit_bank("values", vt, mt)
             product(values[vt, mt], 1, vt, mt, range(D))
-            if vt not in dens:
+            if mt == 0:
                 dens[vt] = banks.tile([P, M_TILES, P], F32, name="den%d" % vt, tag="den%d" % (vt % 2))
             sum_transposed(dens[vt][:, mt, :], weights[vt, mt])
 
-        for vt in range(V_TILES):
-            copy_scores(vt)
         def square(vt):
             nc.scalar.activation(den_squared[:, :, vt, :], dens[vt][:], ACT.Square)
 
-        maximum(0, 1)
-        maximum(0, 0)
-        weigh(0, 1)
-        weigh(0, 0)
-        maximum(1, 0)
-        maximum(1, 1)
-        maximum(2, 0)
-        weigh(1, 0)
-        weigh(1, 1)
-        maximum(2, 1)
-        weigh(2, 0)
-        weigh(2, 1)
-        square(0)
-        square(1)
-        copied_values = {}
-        for unit in GPSIMD_PRODUCTS:
-            copied_values[unit] = keep.tile([P, D, P], F32, name="copied_values%d_%d" % unit)
-            nc.scalar.copy(copied_values[unit][:], values[unit][:])
+        maximum(*units[0])
+        for u, (vt, mt) in enumerate(units):
+            if u + 1 < len(units):
+                maximum(*units[u + 1])
+            weigh(vt, mt)
+            if mt == 0 and vt > 0:
+                square(vt - 1)
 
-        held = shifted_last[:].rearrange("p a d m -> p (a d m)")[:, 2 * P : 6 * P]
-        nc.scalar.activation(held.rearrange("p (mt vt v) -> p mt vt v", mt=M_TILES, vt=last), den_squared[:, :, 0:last, :], ACT.Abs_reciprocal_sqrt)
+        held = shifted[units[-1]][:].rearrange("p d m -> p (d m)")
+        nc.scalar.activation(
+            held.rearrange("p (mt vt v) -> p mt vt v", mt=M_TILES, vt=last), den_squared[:, :, 0:last, :],
+            ACT.Abs_reciprocal_sqrt,
+        )
         square(last)
         inverse_last = keep.tile([P, M_TILES, P], F32, name="inverse_last")
         nc.scalar.activation(inverse_last[:], den_squared[:, :, last, :], ACT.Abs_reciprocal_sqrt)
 
-        num_early = banks.tile([P, M_TILES, last, P], F32, name="num_early", tag="bank0_0")
-        num_last = banks.tile([P, M_TILES, P], F32, name="num_last", tag="bank0_1")
-        for vt, mt in ((0, 1), (1, 0), (1, 1), (0, 0), (2, 0), (2, 1)):
+        num_early = banks.tile([P, M_TILES, last, P], F32, name="num_early", tag="den1")
+        num_last = banks.tile([P, M_TILES, P], F32, name="num_last", tag="bank0_0")
+        for vt, mt in units:
             weighted = keep.tile([P, D, P], F32, name="weighted%d_%d" % (vt, mt))
-            if (vt, mt) in copied_values:
-                nc.gpsimd.tensor_tensor(weighted[:], copied_values[vt, mt][:], weights[vt, mt][:], ALU.mult)
-            else:
-                nc.vector.tensor_tensor(weighted[:], values[vt, mt][:], weights[vt, mt][:], ALU.mult)
+            nc.vector.tensor_tensor(weighted[:], values[vt, mt][:], weights[vt, mt][:], ALU.mult)
             sum_transposed(num_early[:, mt, vt, :] if vt < last else num_last[:, mt, :], weighted)
 
         out_tiles = out.rearrange("(mt p) v -> p mt v", p=P)

@@ -122,9 +122,15 @@ def tile_picked_apool_relu_e_kernel(
         units = [(vt, mt) for vt in range(V_TILES) for mt in range(M_TILES)]
         last = V_TILES - 1
         scores = {unit: unit_bank("scores", *unit) for unit in units}
-        for pieces in ((0, 1), (2, 3)):
-            for vt, mt in units:
+        for vt, pieces in ((0, (0, 1)), (1, (0, 1)), (0, (2, 3)), (1, (2, 3)), (2, (0, 1, 2, 3))):
+            for mt in range(M_TILES):
                 product(scores[vt, mt], 0, vt, mt, pieces)
+
+        rounded = {}
+        for vt in range(1, V_TILES):
+            rounded[vt] = keep.tile([P, M_TILES, D, P], BF16, name="rounded%d" % vt)
+            for mt in range(M_TILES):
+                nc.scalar.copy(rounded[vt][:, mt, :, :], scores[vt, mt][:])
 
         dens = {}
         den_squared = keep.tile([P, M_TILES, V_TILES, P], F32, name="den_squared")
@@ -134,14 +140,29 @@ def tile_picked_apool_relu_e_kernel(
         values = {}
 
         def maximum(vt, mt):
-            largest[vt, mt] = keep.tile([P, P], F32, name="largest%d_%d" % (vt, mt))
+            reduced = keep.tile([P, P], F32, name="largest%d_%d" % (vt, mt))
             nc.vector.tensor_reduce(
-                largest[vt, mt][:], scores[vt, mt][:].rearrange("p d m -> p m d"), mybir.AxisListType.X, ALU.max
+                reduced[:], scores[vt, mt][:].rearrange("p d m -> p m d"), mybir.AxisListType.X, ALU.max
             )
+            largest[vt, mt] = reduced[:]
+
+        pairs = {}
+
+        def maximum_of_pairs(vt):
+            pairs[vt] = keep.tile([P, M_TILES, D // 2, P], BF16, name="pairs%d" % vt)
+            nc.vector.tensor_tensor(
+                pairs[vt][:], rounded[vt][:, :, 0 : D // 2, :], rounded[vt][:, :, D // 2 : D, :], ALU.max
+            )
+
+        def maximum_of_four(vt):
+            reduced = keep.tile([P, M_TILES, P], BF16, name="largest%d" % vt)
+            nc.vector.tensor_tensor(reduced[:], pairs[vt][:, :, 0, :], pairs[vt][:, :, 1, :], ALU.max)
+            for mt in range(M_TILES):
+                largest[vt, mt] = reduced[:, mt, :]
 
         def weigh(vt, mt):
             shifted[vt, mt] = keep.tile([P, D, P], F32, name="shifted%d_%d" % (vt, mt))
-            spread = largest[vt, mt][:].unsqueeze(1).broadcast_to([P, D, P])
+            spread = largest[vt, mt].unsqueeze(1).broadcast_to([P, D, P])
             nc.vector.tensor_tensor(shifted[vt, mt][:], scores[vt, mt][:], spread, ALU.subtract)
             weights[vt, mt] = keep.tile([P, D, P], F32, name="weights%d_%d" % (vt, mt))
             nc.scalar.activation(weights[vt, mt][:], shifted[vt, mt][:], ACT.Exp)
@@ -154,13 +175,20 @@ def tile_picked_apool_relu_e_kernel(
         def square(vt):
             nc.scalar.activation(den_squared[:, :, vt, :], dens[vt][:], ACT.Square)
 
-        maximum(*units[0])
-        for u, (vt, mt) in enumerate(units):
-            if u + 1 < len(units):
-                maximum(*units[u + 1])
-            weigh(vt, mt)
-            if mt == 0 and vt > 0:
-                square(vt - 1)
+        maximum(0, 0)
+        maximum(0, 1)
+        weigh(0, 0)
+        maximum_of_pairs(1)
+        weigh(0, 1)
+        maximum_of_four(1)
+        maximum_of_pairs(2)
+        weigh(1, 0)
+        maximum_of_four(2)
+        weigh(1, 1)
+        square(0)
+        weigh(2, 0)
+        weigh(2, 1)
+        square(1)
 
         held = shifted[units[-1]][:].rearrange("p d m -> p (d m)")
         nc.scalar.activation(
@@ -171,11 +199,13 @@ def tile_picked_apool_relu_e_kernel(
         inverse_last = keep.tile([P, M_TILES, P], F32, name="inverse_last")
         nc.scalar.activation(inverse_last[:], den_squared[:, :, last, :], ACT.Abs_reciprocal_sqrt)
 
-        num_early = banks.tile([P, M_TILES, last, P], F32, name="num_early", tag="den1")
-        num_last = banks.tile([P, M_TILES, P], F32, name="num_last", tag="bank0_0")
         for vt, mt in units:
             weighted = keep.tile([P, D, P], F32, name="weighted%d_%d" % (vt, mt))
             nc.vector.tensor_tensor(weighted[:], values[vt, mt][:], weights[vt, mt][:], ALU.mult)
+            if (vt, mt) == (0, 0):
+                num_early = banks.tile([P, M_TILES, last, P], F32, name="num_early", tag="bank0_0")
+            if (vt, mt) == (last, 0):
+                num_last = banks.tile([P, M_TILES, P], F32, name="num_last", tag="bank0_1")
             sum_transposed(num_early[:, mt, vt, :] if vt < last else num_last[:, mt, :], weighted)
 
         out_tiles = out.rearrange("(mt p) v -> p mt v", p=P)

@@ -20,6 +20,7 @@ ACT = mybir.ActivationFunctionType
 
 P = 128
 PACK = 4
+PAIR = 2
 V_TILES = V // P
 M_TILES = N // P
 
@@ -30,7 +31,10 @@ LOAD_WIDTHS = (
     (2048, 1024, 512, 256, 256),
 )
 LOAD_ORDER = (2, 0, 1, 3)
-QUANTISE_RUNS = ((0, 256), (256, 512), (768, 128), (1152, 128), (896, 256), (1280, 256))
+QUANTISE_RUNS = (
+    (0, 256), (384, 256), (768, 128), (1152, 128), (896, 128), (1280, 128), (256, 128), (640, 128), (1024, 128), (1408, 128)
+)
+WARM_PASSES = 6
 VECTOR_SHARES = (512, 512, 768, 768)
 
 
@@ -61,7 +65,7 @@ def tile_picked_apool_relu_e_kernel(
         picked = keep.tile([P, S, PACK], BF16, name="picked", align_bytes=64)
         for j, widths in zip(LOAD_ORDER, LOAD_WIDTHS):
             row = keep.tile([P, T], F32, name="row%d" % j)
-            row_bf16 = keep.tile([P, T], BF16, name="row_bf16_%d" % j)
+            row_bf16 = keep.tile([P, T], BF16, name="row_bf16_%d" % j, align_bytes=64)
             first = 0
             for width in widths:
                 cols = slice(first, first + width)
@@ -73,6 +77,12 @@ def tile_picked_apool_relu_e_kernel(
                     nc.scalar.copy(row_bf16[:, cols], row[:, cols])
                 else:
                     nc.vector.tensor_copy(row_bf16[:, cols], row[:, cols])
+            if j == LOAD_ORDER[0]:
+                warm_codes = keep.tile([P, P], U32, name="warm_codes", align_bytes=64)
+                warm_scales = keep.tile([P, P], U8, name="warm_scales", align_bytes=64)
+                nc.vector.quantize_mx(
+                    out=warm_codes[:].bitcast(FP8X4), scales=warm_scales[:], in_=row_bf16[:, 0 : PACK * P]
+                )
             share = VECTOR_SHARES[j]
             nc.vector.tensor_copy(picked[:, 0:share, j], row[:].indirect(offsets[:, 0 : share // 16]))
             nc.scalar.activation(
@@ -81,6 +91,18 @@ def tile_picked_apool_relu_e_kernel(
 
         for w, words in enumerate((w1_words, w2_words)):
             nc.sync.dma_start(w_words[:, w, :].bitcast(I32), words[0].bitcast(I32))
+
+        warm_bank = banks.tile([P, N], F32, name="warm_bank", tag="den1")
+        for warm_pass in range(WARM_PASSES):
+            nc.tensor.matmul_mx(
+                out=warm_bank[:],
+                lhsT=warm_codes[:].bitcast(FP8X4),
+                lhsT_scale=warm_scales[:],
+                rhs=w_words[:, 0, :].bitcast(FP4X4),
+                rhs_scale=w_scales[:, 0:N],
+                start=True,
+                stop=True,
+            )
 
         codes = {}
         code_scales = {}
@@ -97,90 +119,77 @@ def tile_picked_apool_relu_e_kernel(
                 codes[entry % V // P, entry // V] = run_codes[:, cols]
                 code_scales[entry % V // P, entry // V] = run_scales[:, cols]
 
-        def product(bank, w, vt, mt, pieces):
-            for d in pieces:
+        def product(bank, w, vt, half):
+            for i in range(PAIR):
                 nc.tensor.matmul_mx(
-                    out=bank[:, d, :],
-                    lhsT=codes[vt, d].bitcast(FP8X4),
-                    lhsT_scale=code_scales[vt, d],
-                    rhs=w_words[:, w, 2 * P * mt : 2 * P * (mt + 1)].bitcast(FP4X4),
-                    rhs_scale=w_scales[:, w * N + P * mt : w * N + P * (mt + 1)],
+                    out=bank[:, i, :],
+                    lhsT=codes[vt, PAIR * half + i].bitcast(FP8X4),
+                    lhsT_scale=code_scales[vt, PAIR * half + i],
+                    rhs=w_words[:, w, :].bitcast(FP4X4),
+                    rhs_scale=w_scales[:, w * N : (w + 1) * N],
                     start=True,
                     stop=True,
                 )
 
-        def sum_transposed(total, terms):
-            for d in range(D):
+        def add_transposed(total, terms, start, stop):
+            steps = [(mt, i) for mt in range(M_TILES) for i in range(PAIR)]
+            for mt, i in steps:
                 nc.tensor.matmul(
-                    total, lhsT=terms[:, d, :], rhs=identity[:], is_transpose=True,
-                    start=(d == 0), stop=(d == D - 1),
+                    total[:, mt, :], lhsT=terms[:, i, mt * P : (mt + 1) * P], rhs=identity[:], is_transpose=True,
+                    start=start and (mt, i) == steps[0], stop=stop and (mt, i) == steps[-1],
                 )
 
-        def unit_bank(name, vt, mt):
-            return banks.tile([P, D, P], F32, name="%s%d_%d" % (name, vt, mt), tag="bank%d_%d" % (vt, mt))
+        def unit_bank(name, vt, half):
+            return banks.tile([P, PAIR, N], F32, name="%s%d_%d" % (name, vt, half), tag="bank%d_%d" % (vt, half))
 
-        units = [(vt, mt) for vt in range(V_TILES) for mt in range(M_TILES)]
+        units = [(vt, half) for vt in range(V_TILES) for half in range(D // PAIR)]
         last = V_TILES - 1
         scores = {unit: unit_bank("scores", *unit) for unit in units}
-        for vt, pieces in ((0, (0, 1)), (1, (0, 1)), (0, (2, 3)), (1, (2, 3)), (2, (0, 1, 2, 3))):
-            for mt in range(M_TILES):
-                product(scores[vt, mt], 0, vt, mt, pieces)
-
         rounded = {}
-        for vt in range(1, V_TILES):
-            rounded[vt] = keep.tile([P, M_TILES, D, P], BF16, name="rounded%d" % vt)
-            for mt in range(M_TILES):
-                nc.scalar.copy(rounded[vt][:, mt, :, :], scores[vt, mt][:])
+        for vt, half in ((0, 0), (1, 0), (0, 1), (1, 1), (2, 0), (2, 1)):
+            product(scores[vt, half], 0, vt, half)
+            if half == 0 or vt == last:
+                rounded[vt, half] = keep.tile([P, PAIR, N], BF16, name="rounded%d_%d" % (vt, half))
+                nc.scalar.copy(rounded[vt, half][:], scores[vt, half][:])
 
         dens = {}
         den_squared = keep.tile([P, M_TILES, V_TILES, P], F32, name="den_squared")
+        pairs = {}
         largest = {}
         shifted = {}
         weights = {}
         values = {}
 
-        def maximum(vt, mt):
-            reduced = keep.tile([P, P], F32, name="largest%d_%d" % (vt, mt))
-            nc.vector.tensor_reduce(
-                reduced[:], scores[vt, mt][:].rearrange("p d m -> p m d"), mybir.AxisListType.X, ALU.max
-            )
-            largest[vt, mt] = reduced[:]
-
-        pairs = {}
-
         def maximum_of_pairs(vt):
-            pairs[vt] = keep.tile([P, M_TILES, D // 2, P], BF16, name="pairs%d" % vt)
-            nc.vector.tensor_tensor(
-                pairs[vt][:], rounded[vt][:, :, 0 : D // 2, :], rounded[vt][:, :, D // 2 : D, :], ALU.max
-            )
+            pairs[vt] = keep.tile([P, PAIR, N], BF16, name="pairs%d" % vt)
+            upper = rounded[vt, 1] if (vt, 1) in rounded else scores[vt, 1]
+            nc.vector.tensor_tensor(pairs[vt][:], upper[:], rounded[vt, 0][:], ALU.max)
 
         def maximum_of_four(vt):
-            reduced = keep.tile([P, M_TILES, P], BF16, name="largest%d" % vt)
-            nc.vector.tensor_tensor(reduced[:], pairs[vt][:, :, 0, :], pairs[vt][:, :, 1, :], ALU.max)
-            for mt in range(M_TILES):
-                largest[vt, mt] = reduced[:, mt, :]
+            largest[vt] = keep.tile([P, N], BF16, name="largest%d" % vt)
+            nc.vector.tensor_tensor(largest[vt][:], pairs[vt][:, 0, :], pairs[vt][:, 1, :], ALU.max)
 
-        def weigh(vt, mt):
-            shifted[vt, mt] = keep.tile([P, D, P], F32, name="shifted%d_%d" % (vt, mt))
-            spread = largest[vt, mt].unsqueeze(1).broadcast_to([P, D, P])
-            nc.vector.tensor_tensor(shifted[vt, mt][:], scores[vt, mt][:], spread, ALU.subtract)
-            weights[vt, mt] = keep.tile([P, D, P], F32, name="weights%d_%d" % (vt, mt))
-            nc.scalar.activation(weights[vt, mt][:], shifted[vt, mt][:], ACT.Exp)
-            values[vt, mt] = unit_bank("values", vt, mt)
-            product(values[vt, mt], 1, vt, mt, range(D))
-            if mt == 0:
+        def weigh(vt, half):
+            shifted[vt, half] = keep.tile([P, PAIR, N], F32, name="shifted%d_%d" % (vt, half))
+            spread = largest[vt][:].unsqueeze(1).broadcast_to([P, PAIR, N])
+            nc.vector.tensor_tensor(shifted[vt, half][:], scores[vt, half][:], spread, ALU.subtract)
+            weights[vt, half] = keep.tile([P, PAIR, N], F32, name="weights%d_%d" % (vt, half))
+            nc.scalar.activation(weights[vt, half][:], shifted[vt, half][:], ACT.Exp)
+            values[vt, half] = unit_bank("values", vt, half)
+            product(values[vt, half], 1, vt, half)
+            if half == 0:
                 dens[vt] = banks.tile([P, M_TILES, P], F32, name="den%d" % vt, tag="den%d" % (vt % 2))
-            sum_transposed(dens[vt][:, mt, :], weights[vt, mt])
+            add_transposed(dens[vt], weights[vt, half], half == 0, half == 1)
 
         def square(vt):
             nc.scalar.activation(den_squared[:, :, vt, :], dens[vt][:], ACT.Square)
 
-        maximum(0, 0)
-        maximum(0, 1)
-        weigh(0, 0)
+        maximum_of_pairs(0)
         maximum_of_pairs(1)
-        weigh(0, 1)
+        maximum_of_four(0)
         maximum_of_four(1)
+        weigh(0, 0)
+        weigh(0, 1)
         maximum_of_pairs(2)
         weigh(1, 0)
         maximum_of_four(2)
@@ -190,7 +199,7 @@ def tile_picked_apool_relu_e_kernel(
         weigh(2, 1)
         square(1)
 
-        held = shifted[units[-1]][:].rearrange("p d m -> p (d m)")
+        held = shifted[units[-1]][:].rearrange("p i n -> p (i n)")
         nc.scalar.activation(
             held.rearrange("p (mt vt v) -> p mt vt v", mt=M_TILES, vt=last), den_squared[:, :, 0:last, :],
             ACT.Abs_reciprocal_sqrt,
@@ -199,14 +208,14 @@ def tile_picked_apool_relu_e_kernel(
         inverse_last = keep.tile([P, M_TILES, P], F32, name="inverse_last")
         nc.scalar.activation(inverse_last[:], den_squared[:, :, last, :], ACT.Abs_reciprocal_sqrt)
 
-        for vt, mt in units:
-            weighted = keep.tile([P, D, P], F32, name="weighted%d_%d" % (vt, mt))
-            nc.vector.tensor_tensor(weighted[:], values[vt, mt][:], weights[vt, mt][:], ALU.mult)
-            if (vt, mt) == (0, 0):
+        for vt, half in units:
+            weighted = keep.tile([P, PAIR, N], F32, name="weighted%d_%d" % (vt, half))
+            nc.vector.tensor_tensor(weighted[:], values[vt, half][:], weights[vt, half][:], ALU.mult)
+            if (vt, half) == (0, 0):
                 num_early = banks.tile([P, M_TILES, last, P], F32, name="num_early", tag="bank0_0")
-            if (vt, mt) == (last, 0):
+            if (vt, half) == (last, 0):
                 num_last = banks.tile([P, M_TILES, P], F32, name="num_last", tag="bank0_1")
-            sum_transposed(num_early[:, mt, vt, :] if vt < last else num_last[:, mt, :], weighted)
+            add_transposed(num_early[:, :, vt, :] if vt < last else num_last, weighted, half == 0, half == 1)
 
         out_tiles = out.rearrange("(mt p) v -> p mt v", p=P)
         result_early = keep.tile([P, M_TILES, last * P], F32, name="result_early")

@@ -31,9 +31,8 @@ LOAD_WIDTHS = (
     (2048, 1024, 512, 256, 256),
 )
 LOAD_ORDER = (2, 0, 1, 3)
-QUANTISE_RUNS = (
-    (0, 256), (384, 256), (768, 128), (1152, 128), (896, 128), (1280, 128), (256, 128), (640, 128), (1024, 128), (1408, 128)
-)
+QUANTISE_RUNS = ((0, 256), (384, 256), (256, 128), (768, 128), (1152, 128), (896, 128), (1280, 128), (640, 128))
+LATE_RUNS = ((1024, 128), (1408, 128))
 WARM_PASSES = 6
 VECTOR_SHARES = (512, 512, 768, 768)
 
@@ -106,7 +105,8 @@ def tile_picked_apool_relu_e_kernel(
 
         codes = {}
         code_scales = {}
-        for first, count in QUANTISE_RUNS:
+
+        def quantise(first, count):
             run_codes = keep.tile([P, count], U32, name="codes%d" % first, align_bytes=64)
             run_scales = keep.tile([P, count], U8, name="code_scales%d" % first, align_bytes=64)
             nc.vector.quantize_mx(
@@ -118,6 +118,9 @@ def tile_picked_apool_relu_e_kernel(
                 cols = slice(entry - first, entry - first + P)
                 codes[entry % V // P, entry // V] = run_codes[:, cols]
                 code_scales[entry % V // P, entry // V] = run_scales[:, cols]
+
+        for run in QUANTISE_RUNS:
+            quantise(*run)
 
         def product(bank, w, vt, half):
             for i in range(PAIR):
@@ -146,11 +149,15 @@ def tile_picked_apool_relu_e_kernel(
         last = V_TILES - 1
         scores = {unit: unit_bank("scores", *unit) for unit in units}
         rounded = {}
-        for vt, half in ((0, 0), (1, 0), (0, 1), (1, 1), (2, 0), (2, 1)):
+
+        def score(vt, half):
             product(scores[vt, half], 0, vt, half)
-            if half == 0 or vt == last:
+            if (vt, half) != (0, 1):
                 rounded[vt, half] = keep.tile([P, PAIR, N], BF16, name="rounded%d_%d" % (vt, half))
                 nc.scalar.copy(rounded[vt, half][:], scores[vt, half][:])
+
+        for unit in ((0, 0), (1, 0), (0, 1), (1, 1), (2, 0)):
+            score(*unit)
 
         dens = {}
         den_squared = keep.tile([P, M_TILES, V_TILES, P], F32, name="den_squared")
@@ -185,14 +192,17 @@ def tile_picked_apool_relu_e_kernel(
             nc.scalar.activation(den_squared[:, :, vt, :], dens[vt][:], ACT.Square)
 
         maximum_of_pairs(0)
-        maximum_of_pairs(1)
+        for run in LATE_RUNS:
+            quantise(*run)
+        score(last, 1)
         maximum_of_four(0)
-        maximum_of_four(1)
+        maximum_of_pairs(1)
         weigh(0, 0)
-        weigh(0, 1)
+        maximum_of_four(1)
         maximum_of_pairs(2)
-        weigh(1, 0)
+        weigh(0, 1)
         maximum_of_four(2)
+        weigh(1, 0)
         weigh(1, 1)
         square(0)
         weigh(2, 0)
@@ -210,7 +220,10 @@ def tile_picked_apool_relu_e_kernel(
 
         for vt, half in units:
             weighted = keep.tile([P, PAIR, N], F32, name="weighted%d_%d" % (vt, half))
-            nc.vector.tensor_tensor(weighted[:], values[vt, half][:], weights[vt, half][:], ALU.mult)
+            for cols in (slice(0, P), slice(P, N)) if (vt, half) == units[-1] else (slice(0, N),):
+                nc.vector.tensor_tensor(
+                    weighted[:, :, cols], values[vt, half][:, :, cols], weights[vt, half][:, :, cols], ALU.mult
+                )
             if (vt, half) == (0, 0):
                 num_early = banks.tile([P, M_TILES, last, P], F32, name="num_early", tag="bank0_0")
             if (vt, half) == (last, 0):

@@ -53,12 +53,15 @@ def tile_picked_apool_relu_e_kernel(
         w_words = keep.tile([P, 2, 2 * N], U8, name="w_words", align_bytes=64)
         w_scales = keep.tile([P, 2 * N], U8, name="w_scales", align_bytes=64)
         nc.gpsimd.memset(w_scales[:].bitcast(I32), 0)
-        for w, scales in enumerate((w1_scales, w2_scales)):
-            for q in range(4):
-                nc.gpsimd.dma_start(
-                    w_scales[32 * q : 32 * q + 4, w * N : (w + 1) * N].bitcast(I32),
-                    scales[0, 4 * q : 4 * q + 4, :].bitcast(I32),
-                )
+
+        def load_scales(queue, w, scales, q):
+            queue.dma_start(
+                w_scales[32 * q : 32 * q + 4, w * N : (w + 1) * N].bitcast(I32),
+                scales[0, 4 * q : 4 * q + 4, :].bitcast(I32),
+            )
+
+        for q in range(4):
+            load_scales(nc.gpsimd, 0, w1_scales, q)
 
         x_rows = xT.rearrange("(p j) t -> j p t", j=PACK)
         picked = keep.tile([P, S, PACK], BF16, name="picked", align_bytes=64)
@@ -88,8 +91,11 @@ def tile_picked_apool_relu_e_kernel(
                 picked[:, share:S, j], row_bf16[:].indirect(offsets[:, share // 16 : S // 16]), ACT.Copy
             )
 
-        for w, words in enumerate((w1_words, w2_words)):
-            nc.sync.dma_start(w_words[:, w, :].bitcast(I32), words[0].bitcast(I32))
+        nc.sync.dma_start(w_words[:, 1, :].bitcast(I32), w2_words[0].bitcast(I32))
+        for q in range(3):
+            load_scales(nc.sync, 1, w2_scales, q)
+        nc.sync.dma_start(w_words[:, 0, :].bitcast(I32), w1_words[0].bitcast(I32))
+        load_scales(nc.sync, 1, w2_scales, 3)
 
         warm_bank = banks.tile([P, N], F32, name="warm_bank", tag="den1")
         for warm_pass in range(WARM_PASSES):

@@ -31,8 +31,9 @@ LOAD_WIDTHS = (
     (2048, 1024, 512, 256, 256),
 )
 LOAD_ORDER = (2, 0, 1, 3)
-QUANTISE_RUNS = ((0, 256), (384, 256), (256, 128), (768, 128), (1152, 128), (896, 128), (1280, 128), (640, 128))
-LATE_RUNS = ((1024, 128), (1408, 128))
+QUANTISE_RUNS = (
+    (0, 256), (384, 256), (768, 128), (1152, 128), (896, 128), (1280, 128), (256, 128), (640, 128), (1024, 128), (1408, 128)
+)
 WARM_PASSES = 6
 VECTOR_SHARES = (512, 512, 768, 768)
 
@@ -155,15 +156,11 @@ def tile_picked_apool_relu_e_kernel(
         last = V_TILES - 1
         scores = {unit: unit_bank("scores", *unit) for unit in units}
         rounded = {}
-
-        def score(vt, half):
+        for vt, half in ((0, 0), (1, 0), (0, 1), (1, 1), (2, 0), (2, 1)):
             product(scores[vt, half], 0, vt, half)
-            if (vt, half) != (0, 1):
+            if half == 0 or vt == last:
                 rounded[vt, half] = keep.tile([P, PAIR, N], BF16, name="rounded%d_%d" % (vt, half))
                 nc.scalar.copy(rounded[vt, half][:], scores[vt, half][:])
-
-        for unit in ((0, 0), (1, 0), (0, 1), (1, 1), (2, 0)):
-            score(*unit)
 
         dens = {}
         den_squared = keep.tile([P, M_TILES, V_TILES, P], F32, name="den_squared")
@@ -198,17 +195,14 @@ def tile_picked_apool_relu_e_kernel(
             nc.scalar.activation(den_squared[:, :, vt, :], dens[vt][:], ACT.Square)
 
         maximum_of_pairs(0)
-        for run in LATE_RUNS:
-            quantise(*run)
-        score(last, 1)
-        maximum_of_four(0)
         maximum_of_pairs(1)
-        weigh(0, 0)
+        maximum_of_four(0)
         maximum_of_four(1)
-        maximum_of_pairs(2)
+        weigh(0, 0)
         weigh(0, 1)
-        maximum_of_four(2)
+        maximum_of_pairs(2)
         weigh(1, 0)
+        maximum_of_four(2)
         weigh(1, 1)
         square(0)
         weigh(2, 0)

@@ -34,7 +34,6 @@ LOAD_ORDER = (2, 0, 1, 3)
 QUANTISE_RUNS = (
     (0, 256), (384, 256), (768, 128), (1152, 128), (896, 128), (1280, 128), (256, 128), (640, 128), (1024, 128), (1408, 128)
 )
-WARM_PASSES = 6
 VECTOR_SHARES = (512, 512, 768, 768)
 
 
@@ -80,12 +79,6 @@ def tile_picked_apool_relu_e_kernel(
                     nc.scalar.copy(row_bf16[:, cols], row[:, cols])
                 else:
                     nc.vector.tensor_copy(row_bf16[:, cols], row[:, cols])
-            if j == LOAD_ORDER[0]:
-                warm_codes = keep.tile([P, P], U32, name="warm_codes", align_bytes=64)
-                warm_scales = keep.tile([P, P], U8, name="warm_scales", align_bytes=64)
-                nc.vector.quantize_mx(
-                    out=warm_codes[:].bitcast(FP8X4), scales=warm_scales[:], in_=row_bf16[:, 0 : PACK * P]
-                )
             share = VECTOR_SHARES[j]
             nc.vector.tensor_copy(picked[:, 0:share, j], row[:].indirect(offsets[:, 0 : share // 16]))
             nc.scalar.activation(
@@ -97,18 +90,6 @@ def tile_picked_apool_relu_e_kernel(
             load_scales(nc.sync, 1, w2_scales, q)
         nc.sync.dma_start(w_words[:, 0, :].bitcast(I32), w1_words[0].bitcast(I32))
         load_scales(nc.sync, 1, w2_scales, 3)
-
-        warm_bank = banks.tile([P, N], F32, name="warm_bank", tag="den1")
-        for warm_pass in range(WARM_PASSES):
-            nc.tensor.matmul_mx(
-                out=warm_bank[:],
-                lhsT=warm_codes[:].bitcast(FP8X4),
-                lhsT_scale=warm_scales[:],
-                rhs=w_words[:, 0, :].bitcast(FP4X4),
-                rhs_scale=w_scales[:, 0:N],
-                start=True,
-                stop=True,
-            )
 
         codes = {}
         code_scales = {}
@@ -163,7 +144,7 @@ def tile_picked_apool_relu_e_kernel(
                 nc.scalar.copy(rounded[vt, half][:], scores[vt, half][:])
 
         dens = {}
-        den_squared = keep.tile([P, M_TILES, V_TILES, P], F32, name="den_squared")
+        den_squared = {}
         pairs = {}
         largest = {}
         shifted = {}
@@ -192,7 +173,8 @@ def tile_picked_apool_relu_e_kernel(
             add_transposed(dens[vt], weights[vt, half], half == 0, half == 1)
 
         def square(vt):
-            nc.scalar.activation(den_squared[:, :, vt, :], dens[vt][:], ACT.Square)
+            den_squared[vt] = keep.tile([P, M_TILES * P], F32, name="den_squared%d" % vt)
+            nc.scalar.activation(den_squared[vt][:], dens[vt][:].rearrange("p mt v -> p (mt v)"), ACT.Square)
 
         maximum_of_pairs(0)
         maximum_of_pairs(1)
@@ -209,37 +191,34 @@ def tile_picked_apool_relu_e_kernel(
         weigh(2, 1)
         square(1)
 
-        held = shifted[units[-1]][:].rearrange("p i n -> p (i n)")
-        nc.scalar.activation(
-            held.rearrange("p (mt vt v) -> p mt vt v", mt=M_TILES, vt=last), den_squared[:, :, 0:last, :],
-            ACT.Abs_reciprocal_sqrt,
-        )
-        square(last)
-        inverse_last = keep.tile([P, M_TILES, P], F32, name="inverse_last")
-        nc.scalar.activation(inverse_last[:], den_squared[:, :, last, :], ACT.Abs_reciprocal_sqrt)
+        held = shifted[units[-1]]
+        inverse_last = keep.tile([P, M_TILES * P], F32, name="inverse_last")
+        inverses = [held[:, 0, :], held[:, 1, :], inverse_last[:]]
 
+        def invert(vt):
+            nc.scalar.activation(inverses[vt], den_squared[vt][:], ACT.Abs_reciprocal_sqrt)
+
+        invert(0)
+        square(last)
+        invert(1)
+        invert(last)
+
+        nums = {}
         for vt, half in units:
             weighted = keep.tile([P, PAIR, N], F32, name="weighted%d_%d" % (vt, half))
             for cols in (slice(0, P), slice(P, N)) if (vt, half) == units[-1] else (slice(0, N),):
                 nc.vector.tensor_tensor(
                     weighted[:, :, cols], values[vt, half][:, :, cols], weights[vt, half][:, :, cols], ALU.mult
                 )
-            if (vt, half) == (0, 0):
-                num_early = banks.tile([P, M_TILES, last, P], F32, name="num_early", tag="bank0_0")
-            if (vt, half) == (last, 0):
-                num_last = banks.tile([P, M_TILES, P], F32, name="num_last", tag="bank0_1")
-            add_transposed(num_early[:, :, vt, :] if vt < last else num_last, weighted, half == 0, half == 1)
+            if half == 0:
+                nums[vt] = banks.tile([P, M_TILES, P], F32, name="num%d" % vt, tag="bank%d_0" % vt)
+            add_transposed(nums[vt], weighted, half == 0, half == 1)
 
         out_tiles = out.rearrange("(mt p) v -> p mt v", p=P)
-        result_early = keep.tile([P, M_TILES, last * P], F32, name="result_early")
-        nc.vector.scalar_tensor_tensor(
-            result_early[:].rearrange("p a b -> p (a b)"), num_early[:].rearrange("p a b c -> p (a b c)"), 0.0,
-            held, ALU.max, ALU.mult,
-        )
-        nc.sync.dma_start(out_tiles[:, :, 0 : last * P], result_early[:])
-        result_last = keep.tile([P, M_TILES, P], F32, name="result_last")
-        nc.vector.scalar_tensor_tensor(
-            result_last[:].rearrange("p a b -> p (a b)"), num_last[:].rearrange("p a b -> p (a b)"), 0.0,
-            inverse_last[:].rearrange("p a b -> p (a b)"), ALU.max, ALU.mult,
-        )
-        nc.sync.dma_start(out_tiles[:, :, last * P : V], result_last[:])
+        for vt in range(V_TILES):
+            result = keep.tile([P, M_TILES, P], F32, name="result%d" % vt)
+            nc.vector.scalar_tensor_tensor(
+                result[:].rearrange("p mt v -> p (mt v)"), nums[vt][:].rearrange("p mt v -> p (mt v)"), 0.0,
+                inverses[vt], ALU.max, ALU.mult,
+            )
+            nc.sync.dma_start(out_tiles[:, :, vt * P : (vt + 1) * P], result[:])

@@ -24,18 +24,6 @@ PAIR = 2
 V_TILES = V // P
 M_TILES = N // P
 
-LOAD_WIDTHS = (
-    (2048, 2048),
-    (2048, 2048),
-    (2048, 1024, 1024),
-    (2048, 1024, 512, 256, 256),
-)
-LOAD_ORDER = (2, 0, 1, 3)
-QUANTISE_RUNS = (
-    (0, 256), (384, 256), (768, 128), (1152, 128), (896, 128), (1280, 128), (256, 128), (640, 128), (1024, 128), (1408, 128)
-)
-VECTOR_SHARES = (512, 512, 768, 768)
-
 
 def tile_picked_apool_relu_e_kernel(
     tc, xT, w1_words, w1_scales, w2_words, w2_scales, offs, out
@@ -46,7 +34,6 @@ def tile_picked_apool_relu_e_kernel(
         banks = ctx.enter_context(tc.psum_pool(name="banks", bufs=1))
 
         offsets = keep.tile([P, S // 16], U16, name="offsets")
-
         identity = keep.tile([P, P], F32, name="identity")
         make_identity(nc, identity[:])
 
@@ -64,63 +51,42 @@ def tile_picked_apool_relu_e_kernel(
             load_scales(nc.gpsimd, 0, w1_scales, q)
 
         x_rows = xT.rearrange("(p j) t -> j p t", j=PACK)
-        picked = keep.tile([P, S, PACK], BF16, name="picked", align_bytes=64)
-        for j, widths in zip(LOAD_ORDER, LOAD_WIDTHS):
-            row = keep.tile([P, T], F32, name="row%d" % j)
-            row_bf16 = keep.tile([P, T], BF16, name="row_bf16_%d" % j, align_bytes=64)
-            first = 0
-            for width in widths:
-                cols = slice(first, first + width)
-                nc.sync.dma_start(row[:, cols], x_rows[j][:, cols])
-                if j == LOAD_ORDER[0] and first == 0:
-                    nc.sync.dma_start(offsets[:], offs)
-                first = first + width
-                if j == PACK - 1 and first == T:
-                    nc.scalar.copy(row_bf16[:, cols], row[:, cols])
-                else:
-                    nc.vector.tensor_copy(row_bf16[:, cols], row[:, cols])
-            share = VECTOR_SHARES[j]
-            nc.vector.tensor_copy(picked[:, 0:share, j], row[:].indirect(offsets[:, 0 : share // 16]))
-            nc.scalar.activation(
-                picked[:, share:S, j], row_bf16[:].indirect(offsets[:, share // 16 : S // 16]), ACT.Copy
-            )
-
-        nc.sync.dma_start(w_words[:, 1, :].bitcast(I32), w2_words[0].bitcast(I32))
-        for q in range(3):
-            load_scales(nc.sync, 1, w2_scales, q)
+        rows = []
+        for j in range(PACK):
+            rows.append(keep.tile([P, T], F32, name="row%d" % j))
+            nc.sync.dma_start(rows[j][:], x_rows[j])
+            if j == 0:
+                nc.sync.dma_start(offsets[:], offs)
         nc.sync.dma_start(w_words[:, 0, :].bitcast(I32), w1_words[0].bitcast(I32))
-        load_scales(nc.sync, 1, w2_scales, 3)
+        nc.sync.dma_start(w_words[:, 1, :].bitcast(I32), w2_words[0].bitcast(I32))
+        for q in range(4):
+            load_scales(nc.sync, 1, w2_scales, q)
+
+        picked = keep.tile([P, V_TILES, D, P, PACK], BF16, name="picked", align_bytes=64)
+
+        def gather(plane, j, first, count):
+            nc.scalar.activation(plane, rows[j][:].indirect(offsets[:, first // 16 : (first + count) // 16]), ACT.Copy)
+
+        by_piece = picked[:].rearrange("p vt d v j -> p d vt v j")
+        for j in range(PACK - 1):
+            plane = keep.tile([P, PAIR, V_TILES, P], BF16, name="plane%d" % j)
+            gather(plane[:].rearrange("p d vt v -> p (d vt v)"), j, PAIR * V, PAIR * V)
+            nc.vector.tensor_copy(by_piece[:, 0:PAIR, :, :, j], rows[j][:].indirect(offsets[:, 0 : PAIR * V // 16]))
+            nc.vector.tensor_copy(by_piece[:, PAIR:D, :, :, j], plane[:])
 
         codes = {}
         code_scales = {}
 
-        def quantise(first, count):
-            run_codes = keep.tile([P, count], U32, name="codes%d" % first, align_bytes=64)
-            run_scales = keep.tile([P, count], U8, name="code_scales%d" % first, align_bytes=64)
-            nc.vector.quantize_mx(
-                out=run_codes[:].bitcast(FP8X4),
-                scales=run_scales[:],
-                in_=picked[:, first : first + count, :].rearrange("p n j -> p (n j)"),
+        def product(bank, w, vt, piece):
+            nc.tensor.matmul_mx(
+                out=bank[:, piece % PAIR, :],
+                lhsT=codes[vt, piece].bitcast(FP8X4),
+                lhsT_scale=code_scales[vt, piece],
+                rhs=w_words[:, w, :].bitcast(FP4X4),
+                rhs_scale=w_scales[:, w * N : (w + 1) * N],
+                start=True,
+                stop=True,
             )
-            for entry in range(first, first + count, P):
-                cols = slice(entry - first, entry - first + P)
-                codes[entry % V // P, entry // V] = run_codes[:, cols]
-                code_scales[entry % V // P, entry // V] = run_scales[:, cols]
-
-        for run in QUANTISE_RUNS:
-            quantise(*run)
-
-        def product(bank, w, vt, half):
-            for i in range(PAIR):
-                nc.tensor.matmul_mx(
-                    out=bank[:, i, :],
-                    lhsT=codes[vt, PAIR * half + i].bitcast(FP8X4),
-                    lhsT_scale=code_scales[vt, PAIR * half + i],
-                    rhs=w_words[:, w, :].bitcast(FP4X4),
-                    rhs_scale=w_scales[:, w * N : (w + 1) * N],
-                    start=True,
-                    stop=True,
-                )
 
         def add_transposed(total, terms, start, stop):
             steps = [(mt, i) for mt in range(M_TILES) for i in range(PAIR)]
@@ -137,88 +103,140 @@ def tile_picked_apool_relu_e_kernel(
         last = V_TILES - 1
         scores = {unit: unit_bank("scores", *unit) for unit in units}
         rounded = {}
-        for vt, half in ((0, 0), (1, 0), (0, 1), (1, 1), (2, 0), (2, 1)):
-            product(scores[vt, half], 0, vt, half)
-            if half == 0 or vt == last:
-                rounded[vt, half] = keep.tile([P, PAIR, N], BF16, name="rounded%d_%d" % (vt, half))
-                nc.scalar.copy(rounded[vt, half][:], scores[vt, half][:])
-
-        dens = {}
-        den_squared = {}
         pairs = {}
         largest = {}
         shifted = {}
         weights = {}
         values = {}
+        dens = {}
+
+        def runs(vt, half):
+            pieces = range(PAIR * half, PAIR * (half + 1))
+            return [range(piece, piece + 1) for piece in pieces] if (vt, half) == units[0] else [pieces]
+
+        def pick_unit(vt, half):
+            planes = []
+            for run in runs(vt, half):
+                planes.append(keep.tile([P, len(run), P], BF16, name="last_plane%d_%d" % (vt, run.start)))
+                for piece in run:
+                    first = piece * V + vt * P
+                    if (vt, half) == units[0]:
+                        window = rows[PACK - 1][:].indirect(offsets[:, first // 16 : (first + P) // 16])
+                        nc.vector.tensor_copy(planes[-1][:, 0, :], window)
+                    else:
+                        gather(planes[-1][:, piece - run.start, :], PACK - 1, first, P)
+            for run, plane in zip(runs(vt, half), planes):
+                nc.vector.tensor_copy(picked[:, vt, run.start : run.stop, :, PACK - 1], plane[:])
+
+        def score(vt, half):
+            words = keep.tile([P, PAIR * P], U32, name="codes%d_%d" % (vt, half), align_bytes=64)
+            scale_bytes = keep.tile([P, PAIR * P], U8, name="code_scales%d_%d" % (vt, half), align_bytes=64)
+            for run in runs(vt, half):
+                cols = slice(run.start % PAIR * P, (run.start % PAIR + len(run)) * P)
+                nc.vector.quantize_mx(
+                    out=words[:, cols].bitcast(FP8X4),
+                    scales=scale_bytes[:, cols],
+                    in_=picked[:, vt, run.start : run.stop, :, :].rearrange("p d n j -> p (d n j)"),
+                )
+                for piece in run:
+                    cols = slice(piece % PAIR * P, (piece % PAIR + 1) * P)
+                    codes[vt, piece] = words[:, cols]
+                    code_scales[vt, piece] = scale_bytes[:, cols]
+                    product(scores[vt, half], 0, vt, piece)
+            rounded[vt, half] = keep.tile([P, PAIR, N], BF16, name="rounded%d_%d" % (vt, half))
+            nc.scalar.copy(rounded[vt, half][:], scores[vt, half][:])
 
         def maximum_of_pairs(vt):
-            pairs[vt] = keep.tile([P, PAIR, N], BF16, name="pairs%d" % vt)
-            upper = rounded[vt, 1] if (vt, 1) in rounded else scores[vt, 1]
-            nc.vector.tensor_tensor(pairs[vt][:], upper[:], rounded[vt, 0][:], ALU.max)
+            pairs[vt] = keep.tile([P, PAIR, N], BF16, name="pairs%d" % vt, tag="pairs%d" % vt)
+            nc.vector.tensor_tensor(pairs[vt][:], rounded[vt, 1][:], rounded[vt, 0][:], ALU.max)
 
         def maximum_of_four(vt):
             largest[vt] = keep.tile([P, N], BF16, name="largest%d" % vt)
             nc.vector.tensor_tensor(largest[vt][:], pairs[vt][:, 0, :], pairs[vt][:, 1, :], ALU.max)
 
+        def shift(vt, half, pieces):
+            if pieces.start == 0:
+                shifted[vt, half] = keep.tile([P, PAIR, N], F32, name="shifted%d_%d" % (vt, half))
+            spread = largest[vt][:].unsqueeze(1).broadcast_to([P, pieces.stop - pieces.start, N])
+            nc.vector.tensor_tensor(shifted[vt, half][:, pieces, :], scores[vt, half][:, pieces, :], spread, ALU.subtract)
+
         def weigh(vt, half):
-            shifted[vt, half] = keep.tile([P, PAIR, N], F32, name="shifted%d_%d" % (vt, half))
-            spread = largest[vt][:].unsqueeze(1).broadcast_to([P, PAIR, N])
-            nc.vector.tensor_tensor(shifted[vt, half][:], scores[vt, half][:], spread, ALU.subtract)
             weights[vt, half] = keep.tile([P, PAIR, N], F32, name="weights%d_%d" % (vt, half))
             nc.scalar.activation(weights[vt, half][:], shifted[vt, half][:], ACT.Exp)
             values[vt, half] = unit_bank("values", vt, half)
-            product(values[vt, half], 1, vt, half)
+            for piece in range(PAIR * half, PAIR * (half + 1)):
+                product(values[vt, half], 1, vt, piece)
+
+        def add_weights(vt, half):
             if half == 0:
-                dens[vt] = banks.tile([P, M_TILES, P], F32, name="den%d" % vt, tag="den%d" % (vt % 2))
+                dens[vt] = banks.tile([P, M_TILES, P], F32, name="den%d" % vt, tag=("den0", "den1", "bank0_0")[vt])
             add_transposed(dens[vt], weights[vt, half], half == 0, half == 1)
 
-        def square(vt):
-            den_squared[vt] = keep.tile([P, M_TILES * P], F32, name="den_squared%d" % vt)
-            nc.scalar.activation(den_squared[vt][:], dens[vt][:].rearrange("p mt v -> p (mt v)"), ACT.Square)
-
+        both, lower, upper = slice(0, PAIR), slice(0, 1), slice(1, PAIR)
+        for vt, half in units[: -D // PAIR]:
+            pick_unit(vt, half)
+            score(vt, half)
+        pick_unit(last, 0)
+        pick_unit(last, 1)
         maximum_of_pairs(0)
-        maximum_of_pairs(1)
+        score(last, 0)
         maximum_of_four(0)
-        maximum_of_four(1)
+        score(last, 1)
+        shift(0, 0, both)
         weigh(0, 0)
+        maximum_of_pairs(1)
+        shift(0, 1, lower)
+        maximum_of_four(1)
+        shift(0, 1, upper)
         weigh(0, 1)
-        maximum_of_pairs(2)
+        shift(1, 0, both)
         weigh(1, 0)
+        maximum_of_pairs(2)
+        shift(1, 1, lower)
         maximum_of_four(2)
+        shift(1, 1, upper)
         weigh(1, 1)
-        square(0)
+        shift(2, 0, both)
         weigh(2, 0)
+        shift(2, 1, both)
         weigh(2, 1)
-        square(1)
 
-        held = shifted[units[-1]]
-        inverse_last = keep.tile([P, M_TILES * P], F32, name="inverse_last")
-        inverses = [held[:, 0, :], held[:, 1, :], inverse_last[:]]
+        for unit in units:
+            add_weights(*unit)
 
-        def invert(vt):
-            nc.scalar.activation(inverses[vt], den_squared[vt][:], ACT.Abs_reciprocal_sqrt)
-
-        invert(0)
-        square(last)
-        invert(1)
-        invert(last)
+        held = shifted[units[-2]]
+        root_first = held[:, 0, :]
+        nc.scalar.activation(root_first, dens[0][:].rearrange("p mt v -> p (mt v)"), ACT.Abs_reciprocal_sqrt)
+        squared_last = keep.tile([P, M_TILES * P], F32, name="squared_last")
+        squares = {1: held[:, 1, :], last: squared_last[:]}
+        inverses = {}
+        for vt in squares:
+            nc.scalar.activation(squares[vt], dens[vt][:].rearrange("p mt v -> p (mt v)"), ACT.Square)
+        for vt in squares:
+            inverses[vt] = keep.tile([P, M_TILES * P], F32, name="inverse%d" % vt)
+            nc.scalar.activation(inverses[vt][:], squares[vt], ACT.Abs_reciprocal_sqrt)
 
         nums = {}
+        products = keep.tile([P, len(units), PAIR, N], F32, name="products", tag="pairs%d" % last)
         for vt, half in units:
-            weighted = keep.tile([P, PAIR, N], F32, name="weighted%d_%d" % (vt, half))
+            weighted = products[:, units.index((vt, half)), :, :]
             for cols in (slice(0, P), slice(P, N)) if (vt, half) == units[-1] else (slice(0, N),):
                 nc.vector.tensor_tensor(
                     weighted[:, :, cols], values[vt, half][:, :, cols], weights[vt, half][:, :, cols], ALU.mult
                 )
             if half == 0:
-                nums[vt] = banks.tile([P, M_TILES, P], F32, name="num%d" % vt, tag="bank%d_0" % vt)
+                nums[vt] = banks.tile([P, M_TILES, P], F32, name="num%d" % vt, tag=("bank0_1", "bank1_0", "bank1_1")[vt])
             add_transposed(nums[vt], weighted, half == 0, half == 1)
 
         out_tiles = out.rearrange("(mt p) v -> p mt v", p=P)
         for vt in range(V_TILES):
             result = keep.tile([P, M_TILES, P], F32, name="result%d" % vt)
-            nc.vector.scalar_tensor_tensor(
-                result[:].rearrange("p mt v -> p (mt v)"), nums[vt][:].rearrange("p mt v -> p (mt v)"), 0.0,
-                inverses[vt], ALU.max, ALU.mult,
-            )
+            flat = result[:].rearrange("p mt v -> p (mt v)")
+            total = nums[vt][:].rearrange("p mt v -> p (mt v)")
+            if vt == 0:
+                once = keep.tile([P, M_TILES * P], F32, name="once")
+                nc.vector.scalar_tensor_tensor(once[:], total, 0.0, root_first, ALU.max, ALU.mult)
+                nc.vector.tensor_tensor(flat, once[:], root_first, ALU.mult)
+            else:
+                nc.vector.scalar_tensor_tensor(flat, total, 0.0, inverses[vt][:], ALU.max, ALU.mult)
             nc.sync.dma_start(out_tiles[:, :, vt * P : (vt + 1) * P], result[:])

@@ -89,7 +89,7 @@ def tile_picked_apool_relu_e_kernel(
             )
 
         def add_transposed(total, terms, start, stop):
-            steps = [(mt, i) for mt in range(M_TILES) for i in range(PAIR)]
+            steps = [(mt, i) for mt in range(total.shape[1]) for i in range(PAIR)]
             for mt, i in steps:
                 nc.tensor.matmul(
                     total[:, mt, :], lhsT=terms[:, i, mt * P : (mt + 1) * P], rhs=identity[:], is_transpose=True,
@@ -157,12 +157,14 @@ def tile_picked_apool_relu_e_kernel(
         def shift(vt, half, pieces):
             if pieces.start == 0:
                 shifted[vt, half] = keep.tile([P, PAIR, N], F32, name="shifted%d_%d" % (vt, half))
+                weights[vt, half] = keep.tile([P, PAIR, N], F32, name="weights%d_%d" % (vt, half))
             spread = largest[vt][:].unsqueeze(1).broadcast_to([P, pieces.stop - pieces.start, N])
             nc.vector.tensor_tensor(shifted[vt, half][:, pieces, :], scores[vt, half][:, pieces, :], spread, ALU.subtract)
 
-        def weigh(vt, half):
-            weights[vt, half] = keep.tile([P, PAIR, N], F32, name="weights%d_%d" % (vt, half))
-            nc.scalar.activation(weights[vt, half][:], shifted[vt, half][:], ACT.Exp)
+        def exponentiate(vt, half, pieces):
+            nc.scalar.activation(weights[vt, half][:, pieces, :], shifted[vt, half][:, pieces, :], ACT.Exp)
+
+        def value_product(vt, half):
             values[vt, half] = unit_bank("values", vt, half)
             for piece in range(PAIR * half, PAIR * (half + 1)):
                 product(values[vt, half], 1, vt, piece)
@@ -183,28 +185,37 @@ def tile_picked_apool_relu_e_kernel(
         maximum_of_four(0)
         score(last, 1)
         shift(0, 0, both)
-        weigh(0, 0)
+        exponentiate(0, 0, both)
+        value_product(0, 0)
         maximum_of_pairs(1)
         shift(0, 1, lower)
         maximum_of_four(1)
         shift(0, 1, upper)
-        weigh(0, 1)
+        exponentiate(0, 1, both)
+        value_product(0, 1)
         shift(1, 0, both)
-        weigh(1, 0)
+        exponentiate(1, 0, both)
+        value_product(1, 0)
         maximum_of_pairs(2)
         shift(1, 1, lower)
+        exponentiate(1, 1, lower)
         maximum_of_four(2)
         shift(1, 1, upper)
-        weigh(1, 1)
-        shift(2, 0, both)
-        weigh(2, 0)
-        shift(2, 1, both)
-        weigh(2, 1)
+        exponentiate(1, 1, upper)
+        value_product(1, 1)
+        for half in range(D // PAIR):
+            for pieces in (lower, upper):
+                shift(last, half, pieces)
+                exponentiate(last, half, pieces)
 
-        for unit in units:
+        for unit in units[: -D // PAIR]:
+            add_weights(*unit)
+        for unit in units[-D // PAIR :]:
+            value_product(*unit)
+        for unit in units[-D // PAIR :]:
             add_weights(*unit)
 
-        held = shifted[units[-2]]
+        held = shifted[units[-1]]
         root_first = held[:, 0, :]
         nc.scalar.activation(root_first, dens[0][:].rearrange("p mt v -> p (mt v)"), ACT.Abs_reciprocal_sqrt)
         squared_last = keep.tile([P, M_TILES * P], F32, name="squared_last")
@@ -216,27 +227,43 @@ def tile_picked_apool_relu_e_kernel(
             inverses[vt] = keep.tile([P, M_TILES * P], F32, name="inverse%d" % vt)
             nc.scalar.activation(inverses[vt][:], squares[vt], ACT.Abs_reciprocal_sqrt)
 
-        nums = {}
         products = keep.tile([P, len(units), PAIR, N], F32, name="products", tag="pairs%d" % last)
-        for vt, half in units:
-            weighted = products[:, units.index((vt, half)), :, :]
-            for cols in (slice(0, P), slice(P, N)) if (vt, half) == units[-1] else (slice(0, N),):
-                nc.vector.tensor_tensor(
-                    weighted[:, :, cols], values[vt, half][:, :, cols], weights[vt, half][:, :, cols], ALU.mult
-                )
+        nums = {}
+
+        def multiply(vt, half, m_tiles, tag):
+            cols = slice(m_tiles.start * P, m_tiles.stop * P)
+            weighted = products[:, units.index((vt, half)), :, cols]
+            nc.vector.tensor_tensor(weighted, values[vt, half][:, :, cols], weights[vt, half][:, :, cols], ALU.mult)
             if half == 0:
-                nums[vt] = banks.tile([P, M_TILES, P], F32, name="num%d" % vt, tag=("bank0_1", "bank1_0", "bank1_1")[vt])
-            add_transposed(nums[vt], weighted, half == 0, half == 1)
+                name = "num%d_%d" % (vt, m_tiles.start)
+                nums[vt, m_tiles.start] = banks.tile([P, len(m_tiles), P], F32, name=name, tag=tag)
+            add_transposed(nums[vt, m_tiles.start], weighted, half == 0, half == 1)
 
         out_tiles = out.rearrange("(mt p) v -> p mt v", p=P)
-        for vt in range(V_TILES):
-            result = keep.tile([P, M_TILES, P], F32, name="result%d" % vt)
-            flat = result[:].rearrange("p mt v -> p (mt v)")
-            total = nums[vt][:].rearrange("p mt v -> p (mt v)")
-            if vt == 0:
-                once = keep.tile([P, M_TILES * P], F32, name="once")
-                nc.vector.scalar_tensor_tensor(once[:], total, 0.0, root_first, ALU.max, ALU.mult)
-                nc.vector.tensor_tensor(flat, once[:], root_first, ALU.mult)
-            else:
-                nc.vector.scalar_tensor_tensor(flat, total, 0.0, inverses[vt][:], ALU.max, ALU.mult)
-            nc.sync.dma_start(out_tiles[:, :, vt * P : (vt + 1) * P], result[:])
+
+        def finish(vt, m_tiles):
+            result = keep.tile([P, len(m_tiles), P], F32, name="result%d_%d" % (vt, m_tiles.start))
+            nc.vector.scalar_tensor_tensor(
+                result[:].rearrange("p mt v -> p (mt v)"), nums[vt, m_tiles.start][:].rearrange("p mt v -> p (mt v)"), 0.0,
+                inverses[vt][:, m_tiles.start * P : m_tiles.stop * P], ALU.max, ALU.mult,
+            )
+            nc.sync.dma_start(out_tiles[:, m_tiles.start : m_tiles.stop, vt * P : (vt + 1) * P], result[:])
+
+        all_m, first_m, second_m = range(M_TILES), range(0, 1), range(1, M_TILES)
+        for vt in range(last):
+            for half in range(D // PAIR):
+                multiply(vt, half, all_m, ("bank0_1", "bank1_0")[vt])
+        multiply(last, 0, first_m, "bank1_1")
+        multiply(last, 0, second_m, "bank2_0")
+        multiply(last, 1, first_m, "bank1_1")
+        once = keep.tile([P, M_TILES * P], F32, name="once")
+        nc.vector.scalar_tensor_tensor(
+            once[:], nums[0, 0][:].rearrange("p mt v -> p (mt v)"), 0.0, root_first, ALU.max, ALU.mult
+        )
+        multiply(last, 1, second_m, "bank2_0")
+        result_first = keep.tile([P, M_TILES, P], F32, name="result_first")
+        nc.vector.tensor_tensor(result_first[:].rearrange("p mt v -> p (mt v)"), once[:], root_first, ALU.mult)
+        nc.sync.dma_start(out_tiles[:, :, 0:P], result_first[:])
+        finish(1, all_m)
+        finish(last, first_m)
+        finish(last, second_m)

@@ -48,7 +48,7 @@ def tile_picked_apool_relu_e_kernel(
             )
 
         for q in range(4):
-            load_scales(nc.gpsimd, 0, w1_scales, q)
+            load_scales(nc.scalar, 0, w1_scales, q)
 
         x_rows = xT.rearrange("(p j) t -> j p t", j=PACK)
         rows = []

@@ -23,6 +23,8 @@ PACK = 4
 PAIR = 2
 V_TILES = V // P
 M_TILES = N // P
+EARLY, LATE = 1, 0
+REFERENCE = D - 1
 
 
 def tile_picked_apool_relu_e_kernel(
@@ -64,29 +66,92 @@ def tile_picked_apool_relu_e_kernel(
 
         picked = keep.tile([P, V_TILES, D, P, PACK], BF16, name="picked", align_bytes=64)
 
-        def gather(plane, j, first, count):
-            nc.scalar.activation(plane, rows[j][:].indirect(offsets[:, first // 16 : (first + count) // 16]), ACT.Copy)
+        def window(j, first, count):
+            return rows[j][:].indirect(offsets[:, first // 16 : (first + count) // 16])
+
+        def gather(plane, j, piece, first, count):
+            sign = -1.0 if piece == REFERENCE else 1.0
+            nc.scalar.activation(plane, window(j, piece * V + first, count), ACT.Copy, scale=sign)
 
         by_piece = picked[:].rearrange("p vt d v j -> p d vt v j")
         for j in range(PACK - 1):
             plane = keep.tile([P, PAIR, V_TILES, P], BF16, name="plane%d" % j)
-            gather(plane[:].rearrange("p d vt v -> p (d vt v)"), j, PAIR * V, PAIR * V)
-            nc.vector.tensor_copy(by_piece[:, 0:PAIR, :, :, j], rows[j][:].indirect(offsets[:, 0 : PAIR * V // 16]))
+            for i in range(PAIR):
+                gather(plane[:, i, :, :].rearrange("p vt v -> p (vt v)"), j, PAIR + i, 0, V)
+            nc.vector.tensor_copy(by_piece[:, 0:PAIR, :, :, j], window(j, 0, PAIR * V))
             nc.vector.tensor_copy(by_piece[:, PAIR:D, :, :, j], plane[:])
 
-        codes = {}
-        code_scales = {}
+        last = V_TILES - 1
+        lower, upper, both = slice(0, 1), slice(1, PAIR), slice(0, PAIR)
+        codes, code_scales, scores, values = {}, {}, {}, {}
+        rounded, partial, largest, shifted, weights, dens = {}, {}, {}, {}, {}, {}
 
-        def product(bank, w, vt, piece):
+        def unit_bank(name, vt, unit):
+            return banks.tile([P, PAIR, N], F32, name="%s%d_%d" % (name, vt, unit), tag="bank%d_%d" % (vt, unit))
+
+        def pick(vt, unit):
+            plane = keep.tile([P, PAIR, P], BF16, name="last_plane%d_%d" % (vt, unit))
+            for i in range(PAIR):
+                if vt == 0 and i == 0:
+                    nc.vector.tensor_copy(plane[:, i, :], window(PACK - 1, PAIR * unit * V, P))
+                else:
+                    gather(plane[:, i, :], PACK - 1, PAIR * unit + i, vt * P, P)
+            nc.vector.tensor_copy(picked[:, vt, PAIR * unit : PAIR * (unit + 1), :, PACK - 1], plane[:])
+
+        def one_pass(target, w, vt, piece, start, stop):
+            cols = slice(piece % PAIR * P, (piece % PAIR + 1) * P)
             nc.tensor.matmul_mx(
-                out=bank[:, piece % PAIR, :],
-                lhsT=codes[vt, piece].bitcast(FP8X4),
-                lhsT_scale=code_scales[vt, piece],
+                out=target,
+                lhsT=codes[vt, piece // PAIR][:, cols].bitcast(FP8X4),
+                lhsT_scale=code_scales[vt, piece // PAIR][:, cols],
                 rhs=w_words[:, w, :].bitcast(FP4X4),
                 rhs_scale=w_scales[:, w * N : (w + 1) * N],
-                start=True,
-                stop=True,
+                start=start,
+                stop=stop,
             )
+
+        def score(vt, unit):
+            codes[vt, unit] = keep.tile([P, PAIR * P], U32, name="codes%d_%d" % (vt, unit), align_bytes=64)
+            code_scales[vt, unit] = keep.tile([P, PAIR * P], U8, name="code_scales%d_%d" % (vt, unit), align_bytes=64)
+            nc.vector.quantize_mx(
+                out=codes[vt, unit][:].bitcast(FP8X4),
+                scales=code_scales[vt, unit][:],
+                in_=picked[:, vt, PAIR * unit : PAIR * (unit + 1), :, :].rearrange("p d n j -> p (d n j)"),
+            )
+            scores[vt, unit] = unit_bank("scores", vt, unit)
+            for piece in range(PAIR * unit, min(PAIR * (unit + 1), REFERENCE)):
+                one_pass(scores[vt, unit][:, piece % PAIR, :], 0, vt, REFERENCE, True, False)
+                one_pass(scores[vt, unit][:, piece % PAIR, :], 0, vt, piece, False, True)
+            shifted[vt, unit] = keep.tile([P, PAIR, N], F32, name="shifted%d_%d" % (vt, unit))
+            weights[vt, unit] = keep.tile([P, PAIR, N], F32, name="weights%d_%d" % (vt, unit))
+            if unit == EARLY:
+                rounded[vt, unit] = keep.tile([P, N], BF16, name="rounded%d_%d" % (vt, unit))
+                nc.scalar.activation(rounded[vt, unit][:], scores[vt, unit][:, 0, :], ACT.Relu)
+            elif vt != last:
+                rounded[vt, unit] = keep.tile([P, PAIR, N], BF16, name="rounded%d_%d" % (vt, unit))
+                nc.scalar.copy(rounded[vt, unit][:], scores[vt, unit][:])
+
+        def late_scores(vt):
+            return scores[vt, LATE] if vt == last else rounded[vt, LATE]
+
+        def first_maximum(vt):
+            partial[vt] = keep.tile([P, N], BF16, name="partial%d" % vt, tag="partial%d" % vt)
+            nc.vector.tensor_tensor(partial[vt][:], late_scores(vt)[:, 0, :], rounded[vt, EARLY][:], ALU.max)
+
+        def second_maximum(vt):
+            largest[vt] = keep.tile([P, N], BF16, name="largest%d" % vt)
+            nc.vector.tensor_tensor(largest[vt][:], late_scores(vt)[:, 1, :], partial[vt][:], ALU.max)
+            nc.scalar.activation(weights[vt, EARLY][:, 1, :], largest[vt][:], ACT.Exp, scale=-1.0)
+
+        def weigh(vt, unit, pieces):
+            spread = largest[vt][:].unsqueeze(1).broadcast_to([P, pieces.stop - pieces.start, N])
+            nc.vector.tensor_tensor(shifted[vt, unit][:, pieces, :], scores[vt, unit][:, pieces, :], spread, ALU.subtract)
+            nc.scalar.activation(weights[vt, unit][:, pieces, :], shifted[vt, unit][:, pieces, :], ACT.Exp)
+
+        def value_product(vt, unit):
+            values[vt, unit] = unit_bank("values", vt, unit)
+            for i in range(PAIR):
+                one_pass(values[vt, unit][:, i, :], 1, vt, PAIR * unit + i, True, True)
 
         def add_transposed(total, terms, start, stop):
             steps = [(mt, i) for mt in range(total.shape[1]) for i in range(PAIR)]
@@ -96,126 +161,69 @@ def tile_picked_apool_relu_e_kernel(
                     start=start and (mt, i) == steps[0], stop=stop and (mt, i) == steps[-1],
                 )
 
-        def unit_bank(name, vt, half):
-            return banks.tile([P, PAIR, N], F32, name="%s%d_%d" % (name, vt, half), tag="bank%d_%d" % (vt, half))
+        for vt in range(last):
+            pick(vt, EARLY)
+            pick(vt, LATE)
+            score(vt, EARLY)
+            score(vt, LATE)
+        pick(last, EARLY)
+        pick(last, LATE)
+        first_maximum(0)
+        score(last, EARLY)
+        second_maximum(0)
+        score(last, LATE)
+        weigh(0, LATE, both)
+        value_product(0, LATE)
+        first_maximum(1)
+        weigh(0, EARLY, lower)
+        value_product(0, EARLY)
+        second_maximum(1)
+        first_maximum(last)
+        weigh(1, LATE, both)
+        value_product(1, LATE)
+        second_maximum(last)
+        weigh(1, EARLY, lower)
+        value_product(1, EARLY)
+        weigh(last, EARLY, lower)
+        weigh(last, LATE, lower)
+        weigh(last, LATE, upper)
 
-        units = [(vt, half) for vt in range(V_TILES) for half in range(D // PAIR)]
-        last = V_TILES - 1
-        scores = {unit: unit_bank("scores", *unit) for unit in units}
-        rounded = {}
-        pairs = {}
-        largest = {}
-        shifted = {}
-        weights = {}
-        values = {}
-        dens = {}
+        def add_weights(vt, tag):
+            dens[vt] = banks.tile([P, M_TILES, P], F32, name="den%d" % vt, tag=tag)
+            order = (EARLY, LATE) if vt == last else (LATE, EARLY)
+            add_transposed(dens[vt], weights[vt, order[0]], True, False)
+            add_transposed(dens[vt], weights[vt, order[1]], False, True)
 
-        def runs(vt, half):
-            pieces = range(PAIR * half, PAIR * (half + 1))
-            return [range(piece, piece + 1) for piece in pieces] if (vt, half) == units[0] else [pieces]
+        add_weights(0, "den0")
+        add_weights(1, "den1")
+        value_product(last, EARLY)
+        value_product(last, LATE)
 
-        def pick_unit(vt, half):
-            planes = []
-            for run in runs(vt, half):
-                planes.append(keep.tile([P, len(run), P], BF16, name="last_plane%d_%d" % (vt, run.start)))
-                for piece in run:
-                    first = piece * V + vt * P
-                    if (vt, half) == units[0]:
-                        window = rows[PACK - 1][:].indirect(offsets[:, first // 16 : (first + P) // 16])
-                        nc.vector.tensor_copy(planes[-1][:, 0, :], window)
-                    else:
-                        gather(planes[-1][:, piece - run.start, :], PACK - 1, first, P)
-            for run, plane in zip(runs(vt, half), planes):
-                nc.vector.tensor_copy(picked[:, vt, run.start : run.stop, :, PACK - 1], plane[:])
+        units = [(vt, unit) for vt in range(V_TILES) for unit in (LATE, EARLY)]
+        products = keep.tile([P, len(units), PAIR, N], F32, name="products", tag="partial%d" % last)
+        nums = {}
 
-        def score(vt, half):
-            words = keep.tile([P, PAIR * P], U32, name="codes%d_%d" % (vt, half), align_bytes=64)
-            scale_bytes = keep.tile([P, PAIR * P], U8, name="code_scales%d_%d" % (vt, half), align_bytes=64)
-            for run in runs(vt, half):
-                cols = slice(run.start % PAIR * P, (run.start % PAIR + len(run)) * P)
-                nc.vector.quantize_mx(
-                    out=words[:, cols].bitcast(FP8X4),
-                    scales=scale_bytes[:, cols],
-                    in_=picked[:, vt, run.start : run.stop, :, :].rearrange("p d n j -> p (d n j)"),
+        def multiply(vt, unit, cols):
+            weighted = products[:, units.index((vt, unit)), :, cols]
+            if unit == LATE:
+                nc.vector.tensor_tensor(weighted, values[vt, unit][:, :, cols], weights[vt, unit][:, :, cols], ALU.mult)
+            else:
+                nc.vector.tensor_tensor(weighted[:, 0, :], values[vt, unit][:, 0, cols], weights[vt, unit][:, 0, cols], ALU.mult)
+                nc.vector.scalar_tensor_tensor(
+                    weighted[:, 1, :], values[vt, unit][:, 1, cols], -1.0, weights[vt, unit][:, 1, cols], ALU.mult, ALU.mult
                 )
-                for piece in run:
-                    cols = slice(piece % PAIR * P, (piece % PAIR + 1) * P)
-                    codes[vt, piece] = words[:, cols]
-                    code_scales[vt, piece] = scale_bytes[:, cols]
-                    product(scores[vt, half], 0, vt, piece)
-            rounded[vt, half] = keep.tile([P, PAIR, N], BF16, name="rounded%d_%d" % (vt, half))
-            nc.scalar.copy(rounded[vt, half][:], scores[vt, half][:])
 
-        def maximum_of_pairs(vt):
-            pairs[vt] = keep.tile([P, PAIR, N], BF16, name="pairs%d" % vt, tag="pairs%d" % vt)
-            nc.vector.tensor_tensor(pairs[vt][:], rounded[vt, 1][:], rounded[vt, 0][:], ALU.max)
+        def add_products(vt, unit, cols, tag):
+            if unit == LATE:
+                shape = [P, (cols.stop - cols.start) // P, P]
+                nums[vt, cols.start] = banks.tile(shape, F32, name="num%d_%d" % (vt, cols.start), tag=tag)
+            add_transposed(nums[vt, cols.start], products[:, units.index((vt, unit)), :, cols], unit == LATE, unit == EARLY)
 
-        def maximum_of_four(vt):
-            largest[vt] = keep.tile([P, N], BF16, name="largest%d" % vt)
-            nc.vector.tensor_tensor(largest[vt][:], pairs[vt][:, 0, :], pairs[vt][:, 1, :], ALU.max)
+        all_cols, first_cols, second_cols = slice(0, N), slice(0, P), slice(P, N)
+        multiply(0, LATE, all_cols)
+        add_weights(last, "bank0_0")
 
-        def shift(vt, half, pieces):
-            if pieces.start == 0:
-                shifted[vt, half] = keep.tile([P, PAIR, N], F32, name="shifted%d_%d" % (vt, half))
-                weights[vt, half] = keep.tile([P, PAIR, N], F32, name="weights%d_%d" % (vt, half))
-            spread = largest[vt][:].unsqueeze(1).broadcast_to([P, pieces.stop - pieces.start, N])
-            nc.vector.tensor_tensor(shifted[vt, half][:, pieces, :], scores[vt, half][:, pieces, :], spread, ALU.subtract)
-
-        def exponentiate(vt, half, pieces):
-            nc.scalar.activation(weights[vt, half][:, pieces, :], shifted[vt, half][:, pieces, :], ACT.Exp)
-
-        def value_product(vt, half):
-            values[vt, half] = unit_bank("values", vt, half)
-            for piece in range(PAIR * half, PAIR * (half + 1)):
-                product(values[vt, half], 1, vt, piece)
-
-        def add_weights(vt, half):
-            if half == 0:
-                dens[vt] = banks.tile([P, M_TILES, P], F32, name="den%d" % vt, tag=("den0", "den1", "bank0_0")[vt])
-            add_transposed(dens[vt], weights[vt, half], half == 0, half == 1)
-
-        both, lower, upper = slice(0, PAIR), slice(0, 1), slice(1, PAIR)
-        for vt, half in units[: -D // PAIR]:
-            pick_unit(vt, half)
-            score(vt, half)
-        pick_unit(last, 0)
-        pick_unit(last, 1)
-        maximum_of_pairs(0)
-        score(last, 0)
-        maximum_of_four(0)
-        score(last, 1)
-        shift(0, 0, both)
-        exponentiate(0, 0, both)
-        value_product(0, 0)
-        maximum_of_pairs(1)
-        shift(0, 1, lower)
-        maximum_of_four(1)
-        shift(0, 1, upper)
-        exponentiate(0, 1, both)
-        value_product(0, 1)
-        shift(1, 0, both)
-        exponentiate(1, 0, both)
-        value_product(1, 0)
-        maximum_of_pairs(2)
-        shift(1, 1, lower)
-        exponentiate(1, 1, lower)
-        maximum_of_four(2)
-        shift(1, 1, upper)
-        exponentiate(1, 1, upper)
-        value_product(1, 1)
-        for half in range(D // PAIR):
-            for pieces in (lower, upper):
-                shift(last, half, pieces)
-                exponentiate(last, half, pieces)
-
-        for unit in units[: -D // PAIR]:
-            add_weights(*unit)
-        for unit in units[-D // PAIR :]:
-            value_product(*unit)
-        for unit in units[-D // PAIR :]:
-            add_weights(*unit)
-
-        held = shifted[units[-1]]
+        held = shifted[last, LATE]
         root_first = held[:, 0, :]
         nc.scalar.activation(root_first, dens[0][:].rearrange("p mt v -> p (mt v)"), ACT.Abs_reciprocal_sqrt)
         squared_last = keep.tile([P, M_TILES * P], F32, name="squared_last")
@@ -227,43 +235,38 @@ def tile_picked_apool_relu_e_kernel(
             inverses[vt] = keep.tile([P, M_TILES * P], F32, name="inverse%d" % vt)
             nc.scalar.activation(inverses[vt][:], squares[vt], ACT.Abs_reciprocal_sqrt)
 
-        products = keep.tile([P, len(units), PAIR, N], F32, name="products", tag="pairs%d" % last)
-        nums = {}
-
-        def multiply(vt, half, m_tiles, tag):
-            cols = slice(m_tiles.start * P, m_tiles.stop * P)
-            weighted = products[:, units.index((vt, half)), :, cols]
-            nc.vector.tensor_tensor(weighted, values[vt, half][:, :, cols], weights[vt, half][:, :, cols], ALU.mult)
-            if half == 0:
-                name = "num%d_%d" % (vt, m_tiles.start)
-                nums[vt, m_tiles.start] = banks.tile([P, len(m_tiles), P], F32, name=name, tag=tag)
-            add_transposed(nums[vt, m_tiles.start], weighted, half == 0, half == 1)
-
         out_tiles = out.rearrange("(mt p) v -> p mt v", p=P)
 
-        def finish(vt, m_tiles):
-            result = keep.tile([P, len(m_tiles), P], F32, name="result%d_%d" % (vt, m_tiles.start))
+        def finish(vt, cols):
+            m_tiles = slice(cols.start // P, cols.stop // P)
+            result = keep.tile([P, m_tiles.stop - m_tiles.start, P], F32, name="result%d_%d" % (vt, cols.start))
             nc.vector.scalar_tensor_tensor(
-                result[:].rearrange("p mt v -> p (mt v)"), nums[vt, m_tiles.start][:].rearrange("p mt v -> p (mt v)"), 0.0,
-                inverses[vt][:, m_tiles.start * P : m_tiles.stop * P], ALU.max, ALU.mult,
+                result[:].rearrange("p mt v -> p (mt v)"), nums[vt, cols.start][:].rearrange("p mt v -> p (mt v)"), 0.0,
+                inverses[vt][:, cols], ALU.max, ALU.mult,
             )
-            nc.sync.dma_start(out_tiles[:, m_tiles.start : m_tiles.stop, vt * P : (vt + 1) * P], result[:])
+            nc.sync.dma_start(out_tiles[:, m_tiles, vt * P : (vt + 1) * P], result[:])
 
-        all_m, first_m, second_m = range(M_TILES), range(0, 1), range(1, M_TILES)
-        for vt in range(last):
-            for half in range(D // PAIR):
-                multiply(vt, half, all_m, ("bank0_1", "bank1_0")[vt])
-        multiply(last, 0, first_m, "bank1_1")
-        multiply(last, 0, second_m, "bank2_0")
-        multiply(last, 1, first_m, "bank1_1")
+        multiply(0, EARLY, all_cols)
+        add_products(0, LATE, all_cols, "bank0_1")
+        add_products(0, EARLY, all_cols, "bank0_1")
+        for unit in (LATE, EARLY):
+            multiply(1, unit, all_cols)
+            add_products(1, unit, all_cols, "bank1_0")
+        multiply(last, LATE, first_cols)
+        add_products(last, LATE, first_cols, "bank1_1")
+        multiply(last, LATE, second_cols)
+        add_products(last, LATE, second_cols, "bank2_0")
+        multiply(last, EARLY, first_cols)
+        add_products(last, EARLY, first_cols, "bank1_1")
         once = keep.tile([P, M_TILES * P], F32, name="once")
         nc.vector.scalar_tensor_tensor(
             once[:], nums[0, 0][:].rearrange("p mt v -> p (mt v)"), 0.0, root_first, ALU.max, ALU.mult
         )
-        multiply(last, 1, second_m, "bank2_0")
+        multiply(last, EARLY, second_cols)
+        add_products(last, EARLY, second_cols, "bank2_0")
         result_first = keep.tile([P, M_TILES, P], F32, name="result_first")
         nc.vector.tensor_tensor(result_first[:].rearrange("p mt v -> p (mt v)"), once[:], root_first, ALU.mult)
         nc.sync.dma_start(out_tiles[:, :, 0:P], result_first[:])
-        finish(1, all_m)
-        finish(last, first_m)
-        finish(last, second_m)
+        finish(1, all_cols)
+        finish(last, first_cols)
+        finish(last, second_cols)

@@ -84,10 +84,10 @@ def tile_picked_apool_relu_e_kernel(
         last = V_TILES - 1
         lower, upper, both = slice(0, 1), slice(1, PAIR), slice(0, PAIR)
         codes, code_scales, scores, values = {}, {}, {}, {}
-        rounded, partial, largest, shifted, weights, dens = {}, {}, {}, {}, {}, {}
+        rounded, partial, largest, shifted, weights, dens, nums = {}, {}, {}, {}, {}, {}, {}
 
-        def unit_bank(name, vt, unit):
-            return banks.tile([P, PAIR, N], F32, name="%s%d_%d" % (name, vt, unit), tag="bank%d_%d" % (vt, unit))
+        def bank(name, tag):
+            return banks.tile([P, PAIR, N], F32, name=name, tag=tag)
 
         def pick(vt, unit):
             plane = keep.tile([P, PAIR, P], BF16, name="last_plane%d_%d" % (vt, unit))
@@ -110,6 +110,10 @@ def tile_picked_apool_relu_e_kernel(
                 stop=stop,
             )
 
+        def value_pass(vt, piece, target):
+            values[vt, piece] = target
+            one_pass(target, 1, vt, piece, True, True)
+
         def score(vt, unit):
             codes[vt, unit] = keep.tile([P, PAIR * P], U32, name="codes%d_%d" % (vt, unit), align_bytes=64)
             code_scales[vt, unit] = keep.tile([P, PAIR * P], U8, name="code_scales%d_%d" % (vt, unit), align_bytes=64)
@@ -118,10 +122,12 @@ def tile_picked_apool_relu_e_kernel(
                 scales=code_scales[vt, unit][:],
                 in_=picked[:, vt, PAIR * unit : PAIR * (unit + 1), :, :].rearrange("p d n j -> p (d n j)"),
             )
-            scores[vt, unit] = unit_bank("scores", vt, unit)
+            scores[vt, unit] = bank("scores%d_%d" % (vt, unit), "bank%d_%d" % (vt, unit))
             for piece in range(PAIR * unit, min(PAIR * (unit + 1), REFERENCE)):
                 one_pass(scores[vt, unit][:, piece % PAIR, :], 0, vt, REFERENCE, True, False)
                 one_pass(scores[vt, unit][:, piece % PAIR, :], 0, vt, piece, False, True)
+            if (vt, unit) == (last, EARLY):
+                value_pass(vt, REFERENCE, scores[vt, unit][:, 1, :])
             shifted[vt, unit] = keep.tile([P, PAIR, N], F32, name="shifted%d_%d" % (vt, unit))
             weights[vt, unit] = keep.tile([P, PAIR, N], F32, name="weights%d_%d" % (vt, unit))
             if unit == EARLY:
@@ -148,18 +154,24 @@ def tile_picked_apool_relu_e_kernel(
             nc.vector.tensor_tensor(shifted[vt, unit][:, pieces, :], scores[vt, unit][:, pieces, :], spread, ALU.subtract)
             nc.scalar.activation(weights[vt, unit][:, pieces, :], shifted[vt, unit][:, pieces, :], ACT.Exp)
 
-        def value_product(vt, unit):
-            values[vt, unit] = unit_bank("values", vt, unit)
+        def value_product(vt, unit, tag):
+            values[vt, "bank", unit] = bank("values%d_%d" % (vt, unit), tag)
             for i in range(PAIR):
-                one_pass(values[vt, unit][:, i, :], 1, vt, PAIR * unit + i, True, True)
+                value_pass(vt, PAIR * unit + i, values[vt, "bank", unit][:, i, :])
 
         def add_transposed(total, terms, start, stop):
-            steps = [(mt, i) for mt in range(total.shape[1]) for i in range(PAIR)]
+            steps = [(mt, i) for mt in range(total.shape[1]) for i in range(terms.shape[1])]
             for mt, i in steps:
                 nc.tensor.matmul(
                     total[:, mt, :], lhsT=terms[:, i, mt * P : (mt + 1) * P], rhs=identity[:], is_transpose=True,
                     start=start and (mt, i) == steps[0], stop=stop and (mt, i) == steps[-1],
                 )
+
+        def add_weights(vt, total):
+            dens[vt] = total
+            order = (EARLY, LATE) if vt == last else (LATE, EARLY)
+            add_transposed(total.rearrange("p (mt v) -> p mt v", v=P), weights[vt, order[0]], True, False)
+            add_transposed(total.rearrange("p (mt v) -> p mt v", v=P), weights[vt, order[1]], False, True)
 
         for vt in range(last):
             pick(vt, EARLY)
@@ -172,65 +184,61 @@ def tile_picked_apool_relu_e_kernel(
         score(last, EARLY)
         second_maximum(0)
         score(last, LATE)
+        value_product(last, LATE, "spare0")
+        shared = bank("shared", "spare1")
+        value_pass(last, PAIR * EARLY, shared[:, 0, :])
         weigh(0, LATE, both)
-        value_product(0, LATE)
+        value_product(0, LATE, "bank0_0")
         first_maximum(1)
         weigh(0, EARLY, lower)
-        value_product(0, EARLY)
+        value_product(0, EARLY, "bank0_1")
         second_maximum(1)
         first_maximum(last)
-        weigh(1, LATE, both)
-        value_product(1, LATE)
+        weigh(1, LATE, lower)
         second_maximum(last)
+        weigh(1, LATE, upper)
+        value_product(1, LATE, "bank1_0")
         weigh(1, EARLY, lower)
-        value_product(1, EARLY)
+        value_product(1, EARLY, "bank1_1")
         weigh(last, EARLY, lower)
         weigh(last, LATE, lower)
         weigh(last, LATE, upper)
 
-        def add_weights(vt, tag):
-            dens[vt] = banks.tile([P, M_TILES, P], F32, name="den%d" % vt, tag=tag)
-            order = (EARLY, LATE) if vt == last else (LATE, EARLY)
-            add_transposed(dens[vt], weights[vt, order[0]], True, False)
-            add_transposed(dens[vt], weights[vt, order[1]], False, True)
+        add_weights(0, shared[:, 1, :])
+        late_dens = bank("late_dens", "bank2_0")
+        add_weights(1, late_dens[:, 0, :])
+        add_weights(last, late_dens[:, 1, :])
 
-        add_weights(0, "den0")
-        add_weights(1, "den1")
-        value_product(last, EARLY)
-        value_product(last, LATE)
+        products = keep.tile([P, V_TILES, D, N], F32, name="products", tag="partial%d" % last)
 
-        units = [(vt, unit) for vt in range(V_TILES) for unit in (LATE, EARLY)]
-        products = keep.tile([P, len(units), PAIR, N], F32, name="products", tag="partial%d" % last)
-        nums = {}
-
-        def multiply(vt, unit, cols):
-            weighted = products[:, units.index((vt, unit)), :, cols]
-            if unit == LATE:
-                nc.vector.tensor_tensor(weighted, values[vt, unit][:, :, cols], weights[vt, unit][:, :, cols], ALU.mult)
+        def multiply(vt, unit, pieces, cols):
+            first = PAIR * unit + pieces.start
+            weighted = products[:, vt, first : PAIR * unit + pieces.stop, cols]
+            if pieces == both:
+                nc.vector.tensor_tensor(weighted, values[vt, "bank", unit][:, :, cols], weights[vt, unit][:, :, cols], ALU.mult)
+            elif first != REFERENCE:
+                nc.vector.tensor_tensor(weighted[:, 0, :], values[vt, first][:, cols], weights[vt, unit][:, pieces.start, cols], ALU.mult)
             else:
-                nc.vector.tensor_tensor(weighted[:, 0, :], values[vt, unit][:, 0, cols], weights[vt, unit][:, 0, cols], ALU.mult)
                 nc.vector.scalar_tensor_tensor(
-                    weighted[:, 1, :], values[vt, unit][:, 1, cols], -1.0, weights[vt, unit][:, 1, cols], ALU.mult, ALU.mult
+                    weighted[:, 0, :], values[vt, first][:, cols], -1.0, weights[vt, unit][:, pieces.start, cols], ALU.mult, ALU.mult
                 )
 
-        def add_products(vt, unit, cols, tag):
-            if unit == LATE:
-                shape = [P, (cols.stop - cols.start) // P, P]
-                nums[vt, cols.start] = banks.tile(shape, F32, name="num%d_%d" % (vt, cols.start), tag=tag)
-            add_transposed(nums[vt, cols.start], products[:, units.index((vt, unit)), :, cols], unit == LATE, unit == EARLY)
+        def add_products(vt, unit, pieces, cols, start, stop):
+            terms = products[:, vt, PAIR * unit + pieces.start : PAIR * unit + pieces.stop, cols]
+            add_transposed(nums[vt, cols.start], terms, start, stop)
 
-        all_cols, first_cols, second_cols = slice(0, N), slice(0, P), slice(P, N)
-        multiply(0, LATE, all_cols)
-        add_weights(last, "bank0_0")
+        def num_bank(vt, cols, tag):
+            shape = [P, (cols.stop - cols.start) // P, P]
+            nums[vt, cols.start] = banks.tile(shape, F32, name="num%d_%d" % (vt, cols.start), tag=tag)
 
         held = shifted[last, LATE]
         root_first = held[:, 0, :]
-        nc.scalar.activation(root_first, dens[0][:].rearrange("p mt v -> p (mt v)"), ACT.Abs_reciprocal_sqrt)
+        nc.scalar.activation(root_first, dens[0], ACT.Abs_reciprocal_sqrt)
         squared_last = keep.tile([P, M_TILES * P], F32, name="squared_last")
         squares = {1: held[:, 1, :], last: squared_last[:]}
         inverses = {}
         for vt in squares:
-            nc.scalar.activation(squares[vt], dens[vt][:].rearrange("p mt v -> p (mt v)"), ACT.Square)
+            nc.scalar.activation(squares[vt], dens[vt], ACT.Square)
         for vt in squares:
             inverses[vt] = keep.tile([P, M_TILES * P], F32, name="inverse%d" % vt)
             nc.scalar.activation(inverses[vt][:], squares[vt], ACT.Abs_reciprocal_sqrt)
@@ -246,24 +254,28 @@ def tile_picked_apool_relu_e_kernel(
             )
             nc.sync.dma_start(out_tiles[:, m_tiles, vt * P : (vt + 1) * P], result[:])
 
-        multiply(0, EARLY, all_cols)
-        add_products(0, LATE, all_cols, "bank0_1")
-        add_products(0, EARLY, all_cols, "bank0_1")
-        for unit in (LATE, EARLY):
-            multiply(1, unit, all_cols)
-            add_products(1, unit, all_cols, "bank1_0")
-        multiply(last, LATE, first_cols)
-        add_products(last, LATE, first_cols, "bank1_1")
-        multiply(last, LATE, second_cols)
-        add_products(last, LATE, second_cols, "bank2_0")
-        multiply(last, EARLY, first_cols)
-        add_products(last, EARLY, first_cols, "bank1_1")
+        all_cols, first_cols, second_cols = slice(0, N), slice(0, P), slice(P, N)
+        for vt in range(last):
+            multiply(vt, LATE, both, all_cols)
+            num_bank(vt, all_cols, ("bank0_0", "bank0_1")[vt])
+            add_products(vt, LATE, both, all_cols, True, False)
+            multiply(vt, EARLY, lower, all_cols)
+            multiply(vt, EARLY, upper, all_cols)
+            add_products(vt, EARLY, both, all_cols, False, True)
+        num_bank(last, first_cols, "bank1_0")
+        num_bank(last, second_cols, "bank1_1")
+        multiply(last, LATE, both, all_cols)
+        multiply(last, EARLY, upper, all_cols)
+        for unit, pieces in ((LATE, both), (EARLY, upper)):
+            for cols in (first_cols, second_cols):
+                add_products(last, unit, pieces, cols, unit == LATE, False)
         once = keep.tile([P, M_TILES * P], F32, name="once")
         nc.vector.scalar_tensor_tensor(
             once[:], nums[0, 0][:].rearrange("p mt v -> p (mt v)"), 0.0, root_first, ALU.max, ALU.mult
         )
-        multiply(last, EARLY, second_cols)
-        add_products(last, EARLY, second_cols, "bank2_0")
+        for cols in (first_cols, second_cols):
+            multiply(last, EARLY, lower, cols)
+            add_products(last, EARLY, lower, cols, False, True)
         result_first = keep.tile([P, M_TILES, P], F32, name="result_first")
         nc.vector.tensor_tensor(result_first[:].rearrange("p mt v -> p (mt v)"), once[:], root_first, ALU.mult)
         nc.sync.dma_start(out_tiles[:, :, 0:P], result_first[:])

@@ -75,7 +75,7 @@ def tile_picked_apool_relu_e_kernel(
 
         by_piece = picked[:].rearrange("p vt d v j -> p d vt v j")
         for j in range(PACK - 1):
-            plane = keep.tile([P, PAIR, V_TILES, P], BF16, name="plane%d" % j)
+            plane = keep.tile([P, PAIR, V_TILES, P], BF16, name="plane%d" % j, tag="plane%d" % j)
             for i in range(PAIR):
                 gather(plane[:, i, :, :].rearrange("p vt v -> p (vt v)"), j, PAIR + i, 0, V)
             nc.vector.tensor_copy(by_piece[:, 0:PAIR, :, :, j], window(j, 0, PAIR * V))
@@ -89,14 +89,22 @@ def tile_picked_apool_relu_e_kernel(
         def bank(name, tag):
             return banks.tile([P, PAIR, N], F32, name=name, tag=tag)
 
-        def pick(vt, unit):
-            plane = keep.tile([P, PAIR, P], BF16, name="last_plane%d_%d" % (vt, unit))
-            for i in range(PAIR):
-                if vt == 0 and i == 0:
-                    nc.vector.tensor_copy(plane[:, i, :], window(PACK - 1, PAIR * unit * V, P))
-                else:
-                    gather(plane[:, i, :], PACK - 1, PAIR * unit + i, vt * P, P)
-            nc.vector.tensor_copy(picked[:, vt, PAIR * unit : PAIR * (unit + 1), :, PACK - 1], plane[:])
+        j_last = PACK - 1
+        planes = {}
+        for vt in range(V_TILES):
+            for unit in (EARLY, LATE):
+                name = "last_plane%d_%d" % (vt, unit)
+                tag = "plane%d" % (j_last - 1) if (vt, unit) == (last, LATE) else name
+                planes[vt, unit] = keep.tile([P, PAIR, P], BF16, name=name, tag=tag)
+
+        def pick(vt, piece):
+            gather(planes[vt, piece // PAIR][:, piece % PAIR, :], j_last, piece, vt * P, P)
+
+        def slots(vt, unit):
+            return picked[:, vt, PAIR * unit : PAIR * (unit + 1), :, j_last]
+
+        def lay(vt, unit):
+            nc.vector.tensor_copy(slots(vt, unit), planes[vt, unit][:])
 
         def one_pass(target, w, vt, piece, start, stop):
             cols = slice(piece % PAIR * P, (piece % PAIR + 1) * P)
@@ -114,39 +122,40 @@ def tile_picked_apool_relu_e_kernel(
             values[vt, piece] = target
             one_pass(target, 1, vt, piece, True, True)
 
-        def score(vt, unit):
-            codes[vt, unit] = keep.tile([P, PAIR * P], U32, name="codes%d_%d" % (vt, unit), align_bytes=64)
-            code_scales[vt, unit] = keep.tile([P, PAIR * P], U8, name="code_scales%d_%d" % (vt, unit), align_bytes=64)
+        def quantise(vt, unit, run):
+            if (vt, unit) not in codes:
+                codes[vt, unit] = keep.tile([P, PAIR * P], U32, name="codes%d_%d" % (vt, unit), align_bytes=64)
+                code_scales[vt, unit] = keep.tile([P, PAIR * P], U8, name="code_scales%d_%d" % (vt, unit), align_bytes=64)
+            cols = slice(run.start * P, run.stop * P)
             nc.vector.quantize_mx(
-                out=codes[vt, unit][:].bitcast(FP8X4),
-                scales=code_scales[vt, unit][:],
-                in_=picked[:, vt, PAIR * unit : PAIR * (unit + 1), :, :].rearrange("p d n j -> p (d n j)"),
+                out=codes[vt, unit][:, cols].bitcast(FP8X4),
+                scales=code_scales[vt, unit][:, cols],
+                in_=picked[:, vt, PAIR * unit + run.start : PAIR * unit + run.stop, :, :].rearrange("p d n j -> p (d n j)"),
             )
-            scores[vt, unit] = bank("scores%d_%d" % (vt, unit), "bank%d_%d" % (vt, unit))
-            for piece in range(PAIR * unit, min(PAIR * (unit + 1), REFERENCE)):
-                one_pass(scores[vt, unit][:, piece % PAIR, :], 0, vt, REFERENCE, True, False)
-                one_pass(scores[vt, unit][:, piece % PAIR, :], 0, vt, piece, False, True)
-            if (vt, unit) == (last, EARLY):
-                value_pass(vt, REFERENCE, scores[vt, unit][:, 1, :])
-            shifted[vt, unit] = keep.tile([P, PAIR, N], F32, name="shifted%d_%d" % (vt, unit))
-            weights[vt, unit] = keep.tile([P, PAIR, N], F32, name="weights%d_%d" % (vt, unit))
-            if unit == EARLY:
-                rounded[vt, unit] = keep.tile([P, N], BF16, name="rounded%d_%d" % (vt, unit))
-                nc.scalar.activation(rounded[vt, unit][:], scores[vt, unit][:, 0, :], ACT.Relu)
-            elif vt != last:
-                rounded[vt, unit] = keep.tile([P, PAIR, N], BF16, name="rounded%d_%d" % (vt, unit))
-                nc.scalar.copy(rounded[vt, unit][:], scores[vt, unit][:])
 
-        def late_scores(vt):
-            return scores[vt, LATE] if vt == last else rounded[vt, LATE]
+        def score_early(vt):
+            for unit in (EARLY, LATE):
+                scores[vt, unit] = bank("scores%d_%d" % (vt, unit), "bank%d_%d" % (vt, unit))
+                shifted[vt, unit] = keep.tile([P, PAIR, N], F32, name="shifted%d_%d" % (vt, unit))
+                weights[vt, unit] = keep.tile([P, PAIR, N], F32, name="weights%d_%d" % (vt, unit))
+            one_pass(scores[vt, EARLY][:, 0, :], 0, vt, REFERENCE, True, False)
+            one_pass(scores[vt, EARLY][:, 0, :], 0, vt, PAIR * EARLY, False, True)
+            for i in range(PAIR):
+                one_pass(scores[vt, LATE][:, i, :], 0, vt, REFERENCE, i == 0, False)
+            rounded[vt] = keep.tile([P, N], BF16, name="rounded%d" % vt)
+            nc.scalar.activation(rounded[vt][:], scores[vt, EARLY][:, 0, :], ACT.Relu)
+
+        def score_late(vt):
+            for i in range(PAIR):
+                one_pass(scores[vt, LATE][:, i, :], 0, vt, PAIR * LATE + i, False, i == PAIR - 1)
 
         def first_maximum(vt):
             partial[vt] = keep.tile([P, N], BF16, name="partial%d" % vt, tag="partial%d" % vt)
-            nc.vector.tensor_tensor(partial[vt][:], late_scores(vt)[:, 0, :], rounded[vt, EARLY][:], ALU.max)
+            nc.vector.tensor_tensor(partial[vt][:], scores[vt, LATE][:, 0, :], rounded[vt][:], ALU.max)
 
         def second_maximum(vt):
             largest[vt] = keep.tile([P, N], BF16, name="largest%d" % vt)
-            nc.vector.tensor_tensor(largest[vt][:], late_scores(vt)[:, 1, :], partial[vt][:], ALU.max)
+            nc.vector.tensor_tensor(largest[vt][:], scores[vt, LATE][:, 1, :], partial[vt][:], ALU.max)
             nc.scalar.activation(weights[vt, EARLY][:, 1, :], largest[vt][:], ACT.Exp, scale=-1.0)
 
         def weigh(vt, unit, pieces):
@@ -173,38 +182,57 @@ def tile_picked_apool_relu_e_kernel(
             add_transposed(total.rearrange("p (mt v) -> p mt v", v=P), weights[vt, order[0]], True, False)
             add_transposed(total.rearrange("p (mt v) -> p mt v", v=P), weights[vt, order[1]], False, True)
 
-        for vt in range(last):
-            pick(vt, EARLY)
-            pick(vt, LATE)
-            score(vt, EARLY)
-            score(vt, LATE)
-        pick(last, EARLY)
-        pick(last, LATE)
+        first_plane = planes[0, EARLY]
+        for i in (1, 0):
+            nc.vector.tensor_copy(first_plane[:, i, :], window(j_last, (PAIR * EARLY + i) * V, P))
+        for vt, piece in ((0, 0), (1, REFERENCE), (0, 1), (1, 2), (1, 0), (1, 1), (last, REFERENCE), (last, 2)):
+            pick(vt, piece)
+        nc.vector.tensor_scalar(slots(0, EARLY)[:, 1, :], first_plane[:, 1, :], -1.0, None, ALU.mult)
+        nc.vector.tensor_copy(slots(0, EARLY)[:, 0, :], first_plane[:, 0, :])
+        quantise(0, EARLY, upper)
+        lay(0, LATE)
+        quantise(0, EARLY, lower)
+        score_early(0)
+        pick(last, 0)
+        pick(last, 1)
+        lay(1, EARLY)
+        quantise(0, LATE, both)
+        score_late(0)
+        quantise(1, EARLY, both)
+        score_early(1)
+        lay(1, LATE)
+        lay(last, EARLY)
+        quantise(1, LATE, both)
+        score_late(1)
+        nc.scalar.copy(slots(last, LATE), planes[last, LATE][:])
         first_maximum(0)
-        score(last, EARLY)
+        quantise(last, EARLY, both)
+        score_early(last)
         second_maximum(0)
-        score(last, LATE)
+        quantise(last, LATE, both)
+        score_late(last)
+        value_pass(last, REFERENCE, scores[last, EARLY][:, 1, :])
         value_product(last, LATE, "spare0")
         shared = bank("shared", "spare1")
         value_pass(last, PAIR * EARLY, shared[:, 0, :])
+        weigh(0, EARLY, lower)
+        first_maximum(1)
         weigh(0, LATE, both)
         value_product(0, LATE, "bank0_0")
-        first_maximum(1)
-        weigh(0, EARLY, lower)
         value_product(0, EARLY, "bank0_1")
+        add_weights(0, shared[:, 1, :])
         second_maximum(1)
         first_maximum(last)
         weigh(1, LATE, lower)
-        second_maximum(last)
         weigh(1, LATE, upper)
-        value_product(1, LATE, "bank1_0")
+        second_maximum(last)
         weigh(1, EARLY, lower)
+        value_product(1, LATE, "bank1_0")
         value_product(1, EARLY, "bank1_1")
         weigh(last, EARLY, lower)
         weigh(last, LATE, lower)
         weigh(last, LATE, upper)
 
-        add_weights(0, shared[:, 1, :])
         late_dens = bank("late_dens", "bank2_0")
         add_weights(1, late_dens[:, 0, :])
         add_weights(last, late_dens[:, 1, :])

@@ -273,14 +273,14 @@ def tile_picked_apool_relu_e_kernel(
 
         out_tiles = out.rearrange("(mt p) v -> p mt v", p=P)
 
-        def finish(vt, cols):
+        def finish(vt, cols, queue):
             m_tiles = slice(cols.start // P, cols.stop // P)
             result = keep.tile([P, m_tiles.stop - m_tiles.start, P], F32, name="result%d_%d" % (vt, cols.start))
             nc.vector.scalar_tensor_tensor(
                 result[:].rearrange("p mt v -> p (mt v)"), nums[vt, cols.start][:].rearrange("p mt v -> p (mt v)"), 0.0,
                 inverses[vt][:, cols], ALU.max, ALU.mult,
             )
-            nc.sync.dma_start(out_tiles[:, m_tiles, vt * P : (vt + 1) * P], result[:])
+            queue.dma_start(out_tiles[:, m_tiles, vt * P : (vt + 1) * P], result[:])
 
         all_cols, first_cols, second_cols = slice(0, N), slice(0, P), slice(P, N)
         for vt in range(last):
@@ -307,6 +307,6 @@ def tile_picked_apool_relu_e_kernel(
         result_first = keep.tile([P, M_TILES, P], F32, name="result_first")
         nc.vector.tensor_tensor(result_first[:].rearrange("p mt v -> p (mt v)"), once[:], root_first, ALU.mult)
         nc.sync.dma_start(out_tiles[:, :, 0:P], result_first[:])
-        finish(1, all_cols)
-        finish(last, first_cols)
-        finish(last, second_cols)
+        finish(1, all_cols, nc.scalar)
+        finish(last, first_cols, nc.sync)
+        finish(last, second_cols, nc.scalar)

from contextlib import ExitStack

import concourse.mybir as mybir
from concourse.masks import make_identity

K, T, S, V, N = 512, 4096, 1536, 384, 256
D = S // V
FLOPS = 2 * 2 * K * N * S

F32 = mybir.dt.float32
BF16 = mybir.dt.bfloat16
I32 = mybir.dt.int32
U32 = mybir.dt.uint32
U16 = mybir.dt.uint16
U8 = mybir.dt.uint8
FP8X4 = mybir.dt.float8_e4m3fn_x4
FP4X4 = mybir.dt.float4_e2m1fn_x4
ALU = mybir.AluOpType
ACT = mybir.ActivationFunctionType

P = 128
PACK = 4
PAIR = 2
V_TILES = V // P
M_TILES = N // P
EARLY, LATE = 1, 0
REFERENCE = D - 1


def tile_picked_apool_relu_e_kernel(
    tc, xT, w1_words, w1_scales, w2_words, w2_scales, offs, out
):
    nc = tc.nc
    with ExitStack() as ctx:
        keep = ctx.enter_context(tc.tile_pool(name="keep", bufs=1))
        banks = ctx.enter_context(tc.psum_pool(name="banks", bufs=1))

        offsets = keep.tile([P, S // 16], U16, name="offsets")
        identity = keep.tile([P, P], F32, name="identity")
        make_identity(nc, identity[:])

        w_words = keep.tile([P, 2, 2 * N], U8, name="w_words", align_bytes=64)
        w_scales = keep.tile([P, 2 * N], U8, name="w_scales", align_bytes=64)
        nc.gpsimd.memset(w_scales[:].bitcast(I32), 0)

        def load_scales(queue, w, scales, q):
            queue.dma_start(
                w_scales[32 * q : 32 * q + 4, w * N : (w + 1) * N].bitcast(I32),
                scales[0, 4 * q : 4 * q + 4, :].bitcast(I32),
            )

        for q in range(4):
            load_scales(nc.scalar, 0, w1_scales, q)

        x_rows = xT.rearrange("(p j) t -> j p t", j=PACK)
        rows = []
        for j in range(PACK):
            rows.append(keep.tile([P, T], F32, name="row%d" % j))
            nc.sync.dma_start(rows[j][:], x_rows[j])
            if j == 0:
                nc.sync.dma_start(offsets[:], offs)
        nc.sync.dma_start(w_words[:, 0, :].bitcast(I32), w1_words[0].bitcast(I32))
        nc.sync.dma_start(w_words[:, 1, :].bitcast(I32), w2_words[0].bitcast(I32))
        for q in range(4):
            load_scales(nc.sync, 1, w2_scales, q)

        picked = keep.tile([P, V_TILES, D, P, PACK], BF16, name="picked", align_bytes=64)

        def window(j, first, count):
            return rows[j][:].indirect(offsets[:, first // 16 : (first + count) // 16])

        def gather(plane, j, piece, first, count):
            sign = -1.0 if piece == REFERENCE else 1.0
            nc.scalar.activation(plane, window(j, piece * V + first, count), ACT.Copy, scale=sign)

        by_piece = picked[:].rearrange("p vt d v j -> p d vt v j")
        for j in range(PACK - 1):
            plane = keep.tile([P, PAIR, V_TILES, P], BF16, name="plane%d" % j, tag="plane%d" % j)
            for i in range(PAIR):
                gather(plane[:, i, :, :].rearrange("p vt v -> p (vt v)"), j, PAIR + i, 0, V)
            nc.vector.tensor_copy(by_piece[:, 0:PAIR, :, :, j], window(j, 0, PAIR * V))
            nc.vector.tensor_copy(by_piece[:, PAIR:D, :, :, j], plane[:])

        last = V_TILES - 1
        lower, upper, both = slice(0, 1), slice(1, PAIR), slice(0, PAIR)
        codes, code_scales, scores, values = {}, {}, {}, {}
        rounded, partial, largest, shifted, weights, dens, nums = {}, {}, {}, {}, {}, {}, {}

        def bank(name, tag):
            return banks.tile([P, PAIR, N], F32, name=name, tag=tag)

        j_last = PACK - 1
        planes = {}
        for vt in range(V_TILES):
            for unit in (EARLY, LATE):
                name = "last_plane%d_%d" % (vt, unit)
                tag = "plane%d" % (j_last - 1) if (vt, unit) == (last, LATE) else name
                planes[vt, unit] = keep.tile([P, PAIR, P], BF16, name=name, tag=tag)

        def pick(vt, piece):
            gather(planes[vt, piece // PAIR][:, piece % PAIR, :], j_last, piece, vt * P, P)

        def slots(vt, unit):
            return picked[:, vt, PAIR * unit : PAIR * (unit + 1), :, j_last]

        def lay(vt, unit):
            nc.vector.tensor_copy(slots(vt, unit), planes[vt, unit][:])

        def one_pass(target, w, vt, piece, start, stop):
            cols = slice(piece % PAIR * P, (piece % PAIR + 1) * P)
            nc.tensor.matmul_mx(
                out=target,
                lhsT=codes[vt, piece // PAIR][:, cols].bitcast(FP8X4),
                lhsT_scale=code_scales[vt, piece // PAIR][:, cols],
                rhs=w_words[:, w, :].bitcast(FP4X4),
                rhs_scale=w_scales[:, w * N : (w + 1) * N],
                start=start,
                stop=stop,
            )

        def value_pass(vt, piece, target):
            values[vt, piece] = target
            one_pass(target, 1, vt, piece, True, True)

        def quantise(vt, unit, run):
            if (vt, unit) not in codes:
                codes[vt, unit] = keep.tile([P, PAIR * P], U32, name="codes%d_%d" % (vt, unit), align_bytes=64)
                code_scales[vt, unit] = keep.tile([P, PAIR * P], U8, name="code_scales%d_%d" % (vt, unit), align_bytes=64)
            cols = slice(run.start * P, run.stop * P)
            nc.vector.quantize_mx(
                out=codes[vt, unit][:, cols].bitcast(FP8X4),
                scales=code_scales[vt, unit][:, cols],
                in_=picked[:, vt, PAIR * unit + run.start : PAIR * unit + run.stop, :, :].rearrange("p d n j -> p (d n j)"),
            )

        def score_early(vt):
            for unit in (EARLY, LATE):
                scores[vt, unit] = bank("scores%d_%d" % (vt, unit), "bank%d_%d" % (vt, unit))
                shifted[vt, unit] = keep.tile([P, PAIR, N], F32, name="shifted%d_%d" % (vt, unit))
                weights[vt, unit] = keep.tile([P, PAIR, N], F32, name="weights%d_%d" % (vt, unit))
            one_pass(scores[vt, EARLY][:, 0, :], 0, vt, REFERENCE, True, False)
            one_pass(scores[vt, EARLY][:, 0, :], 0, vt, PAIR * EARLY, False, True)
            for i in range(PAIR):
                one_pass(scores[vt, LATE][:, i, :], 0, vt, REFERENCE, i == 0, False)
            rounded[vt] = keep.tile([P, N], BF16, name="rounded%d" % vt)
            nc.scalar.activation(rounded[vt][:], scores[vt, EARLY][:, 0, :], ACT.Relu)

        def score_late(vt):
            for i in range(PAIR):
                one_pass(scores[vt, LATE][:, i, :], 0, vt, PAIR * LATE + i, False, i == PAIR - 1)

        def first_maximum(vt):
            partial[vt] = keep.tile([P, N], BF16, name="partial%d" % vt, tag="partial%d" % vt)
            nc.vector.tensor_tensor(partial[vt][:], scores[vt, LATE][:, 0, :], rounded[vt][:], ALU.max)

        def second_maximum(vt):
            largest[vt] = keep.tile([P, N], BF16, name="largest%d" % vt)
            nc.vector.tensor_tensor(largest[vt][:], scores[vt, LATE][:, 1, :], partial[vt][:], ALU.max)
            nc.scalar.activation(weights[vt, EARLY][:, 1, :], largest[vt][:], ACT.Exp, scale=-1.0)

        def weigh(vt, unit, pieces):
            spread = largest[vt][:].unsqueeze(1).broadcast_to([P, pieces.stop - pieces.start, N])
            nc.vector.tensor_tensor(shifted[vt, unit][:, pieces, :], scores[vt, unit][:, pieces, :], spread, ALU.subtract)
            nc.scalar.activation(weights[vt, unit][:, pieces, :], shifted[vt, unit][:, pieces, :], ACT.Exp)

        def value_product(vt, unit, tag):
            values[vt, "bank", unit] = bank("values%d_%d" % (vt, unit), tag)
            for i in range(PAIR):
                value_pass(vt, PAIR * unit + i, values[vt, "bank", unit][:, i, :])

        def add_transposed(total, terms, start, stop):
            steps = [(mt, i) for mt in range(total.shape[1]) for i in range(terms.shape[1])]
            for mt, i in steps:
                nc.tensor.matmul(
                    total[:, mt, :], lhsT=terms[:, i, mt * P : (mt + 1) * P], rhs=identity[:], is_transpose=True,
                    start=start and (mt, i) == steps[0], stop=stop and (mt, i) == steps[-1],
                )

        def add_weights(vt, total):
            dens[vt] = total
            order = (EARLY, LATE) if vt == last else (LATE, EARLY)
            add_transposed(total.rearrange("p (mt v) -> p mt v", v=P), weights[vt, order[0]], True, False)
            add_transposed(total.rearrange("p (mt v) -> p mt v", v=P), weights[vt, order[1]], False, True)

        first_plane = planes[0, EARLY]
        for i in (1, 0):
            nc.vector.tensor_copy(first_plane[:, i, :], window(j_last, (PAIR * EARLY + i) * V, P))
        for vt, piece in ((0, 0), (1, REFERENCE), (0, 1), (1, 2), (1, 0), (1, 1), (last, REFERENCE), (last, 2)):
            pick(vt, piece)
        nc.vector.tensor_scalar(slots(0, EARLY)[:, 1, :], first_plane[:, 1, :], -1.0, None, ALU.mult)
        nc.vector.tensor_copy(slots(0, EARLY)[:, 0, :], first_plane[:, 0, :])
        quantise(0, EARLY, upper)
        lay(0, LATE)
        quantise(0, EARLY, lower)
        score_early(0)
        pick(last, 0)
        pick(last, 1)
        lay(1, EARLY)
        quantise(0, LATE, both)
        score_late(0)
        quantise(1, EARLY, both)
        score_early(1)
        lay(1, LATE)
        lay(last, EARLY)
        quantise(1, LATE, both)
        score_late(1)
        nc.scalar.copy(slots(last, LATE), planes[last, LATE][:])
        first_maximum(0)
        quantise(last, EARLY, both)
        score_early(last)
        second_maximum(0)
        quantise(last, LATE, both)
        score_late(last)
        value_pass(last, REFERENCE, scores[last, EARLY][:, 1, :])
        value_product(last, LATE, "spare0")
        shared = bank("shared", "spare1")
        value_pass(last, PAIR * EARLY, shared[:, 0, :])
        weigh(0, EARLY, lower)
        first_maximum(1)
        weigh(0, LATE, both)
        value_product(0, LATE, "bank0_0")
        value_product(0, EARLY, "bank0_1")
        add_weights(0, shared[:, 1, :])
        second_maximum(1)
        first_maximum(last)
        weigh(1, LATE, lower)
        weigh(1, LATE, upper)
        second_maximum(last)
        weigh(1, EARLY, lower)
        value_product(1, LATE, "bank1_0")
        value_product(1, EARLY, "bank1_1")
        weigh(last, EARLY, lower)
        weigh(last, LATE, lower)
        weigh(last, LATE, upper)

        late_dens = bank("late_dens", "bank2_0")
        add_weights(1, late_dens[:, 0, :])
        add_weights(last, late_dens[:, 1, :])

        products = keep.tile([P, V_TILES, D, N], F32, name="products", tag="partial%d" % last)

        def multiply(vt, unit, pieces, cols):
            first = PAIR * unit + pieces.start
            weighted = products[:, vt, first : PAIR * unit + pieces.stop, cols]
            if pieces == both:
                nc.vector.tensor_tensor(weighted, values[vt, "bank", unit][:, :, cols], weights[vt, unit][:, :, cols], ALU.mult)
            elif first != REFERENCE:
                nc.vector.tensor_tensor(weighted[:, 0, :], values[vt, first][:, cols], weights[vt, unit][:, pieces.start, cols], ALU.mult)
            else:
                nc.vector.scalar_tensor_tensor(
                    weighted[:, 0, :], values[vt, first][:, cols], -1.0, weights[vt, unit][:, pieces.start, cols], ALU.mult, ALU.mult
                )

        def add_products(vt, unit, pieces, cols, start, stop):
            terms = products[:, vt, PAIR * unit + pieces.start : PAIR * unit + pieces.stop, cols]
            add_transposed(nums[vt, cols.start], terms, start, stop)

        def num_bank(vt, cols, tag):
            shape = [P, (cols.stop - cols.start) // P, P]
            nums[vt, cols.start] = banks.tile(shape, F32, name="num%d_%d" % (vt, cols.start), tag=tag)

        held = shifted[last, LATE]
        root_first = held[:, 0, :]
        nc.scalar.activation(root_first, dens[0], ACT.Abs_reciprocal_sqrt)
        squared_last = keep.tile([P, M_TILES * P], F32, name="squared_last")
        squares = {1: held[:, 1, :], last: squared_last[:]}
        inverses = {}
        for vt in squares:
            nc.scalar.activation(squares[vt], dens[vt], ACT.Square)
        for vt in squares:
            inverses[vt] = keep.tile([P, M_TILES * P], F32, name="inverse%d" % vt)
            nc.scalar.activation(inverses[vt][:], squares[vt], ACT.Abs_reciprocal_sqrt)

        out_tiles = out.rearrange("(mt p) v -> p mt v", p=P)

        def finish(vt, cols, queue):
            m_tiles = slice(cols.start // P, cols.stop // P)
            result = keep.tile([P, m_tiles.stop - m_tiles.start, P], F32, name="result%d_%d" % (vt, cols.start))
            nc.vector.scalar_tensor_tensor(
                result[:].rearrange("p mt v -> p (mt v)"), nums[vt, cols.start][:].rearrange("p mt v -> p (mt v)"), 0.0,
                inverses[vt][:, cols], ALU.max, ALU.mult,
            )
            queue.dma_start(out_tiles[:, m_tiles, vt * P : (vt + 1) * P], result[:])

        all_cols, first_cols, second_cols = slice(0, N), slice(0, P), slice(P, N)
        for vt in range(last):
            multiply(vt, LATE, both, all_cols)
            num_bank(vt, all_cols, ("bank0_0", "bank0_1")[vt])
            add_products(vt, LATE, both, all_cols, True, False)
            multiply(vt, EARLY, lower, all_cols)
            multiply(vt, EARLY, upper, all_cols)
            add_products(vt, EARLY, both, all_cols, False, True)
        num_bank(last, first_cols, "bank1_0")
        num_bank(last, second_cols, "bank1_1")
        multiply(last, LATE, both, all_cols)
        multiply(last, EARLY, upper, all_cols)
        for unit, pieces in ((LATE, both), (EARLY, upper)):
            for cols in (first_cols, second_cols):
                add_products(last, unit, pieces, cols, unit == LATE, False)
        once = keep.tile([P, M_TILES * P], F32, name="once")
        nc.vector.scalar_tensor_tensor(
            once[:], nums[0, 0][:].rearrange("p mt v -> p (mt v)"), 0.0, root_first, ALU.max, ALU.mult
        )
        for cols in (first_cols, second_cols):
            multiply(last, EARLY, lower, cols)
            add_products(last, EARLY, lower, cols, False, True)
        result_first = keep.tile([P, M_TILES, P], F32, name="result_first")
        nc.vector.tensor_tensor(result_first[:].rearrange("p mt v -> p (mt v)"), once[:], root_first, ALU.mult)
        nc.sync.dma_start(out_tiles[:, :, 0:P], result_first[:])
        finish(1, all_cols, nc.scalar)
        finish(last, first_cols, nc.sync)
        finish(last, second_cols, nc.scalar)
